import numpy as np
import ml_dtypes


def mxq(x, axis, fmt="e4m3"):
    dtype, down = {"e4m3": (ml_dtypes.float8_e4m3fn, 7), "e5m2": (ml_dtypes.float8_e5m2, 14)}[fmt]
    v = np.moveaxis(np.asarray(x, np.float32).astype(ml_dtypes.bfloat16).astype(np.float64), axis, -1)
    blocks = v.reshape(v.shape[:-1] + (-1, 32))
    amax = np.abs(blocks).max(-1, keepdims=True)
    byte = np.maximum(np.where(amax > 0, np.frexp(amax)[1] - 1 + 127, 0) - down, 1)
    scale = np.exp2(byte - 127.0)
    codes = (blocks / scale).astype(np.float32).astype(dtype).astype(np.float64)
    return np.moveaxis((codes * scale).reshape(v.shape), -1, axis)


WIDE = False


def mx_kscale(k):
    if not WIDE:
        return np.ones(k)
    levels = np.array([10, -10, 5, -5, 0])
    if k % 512:
        return np.exp2(np.random.permutation(np.resize(levels, k // 32))).repeat(32)
    a = np.empty((k // 512, 16))
    for p in range(k // 512):
        a[p, :8] = np.random.permutation(np.resize(levels, 8))
        for g in range(8):
            far = levels[np.abs(levels - a[p, g]) >= 10]
            a[p, g + 8] = far[np.random.randint(len(far))]
    return np.exp2(a.ravel()).repeat(32)


def f64(x):
    return np.asarray(x).astype(np.float64)


def striped(idx):
    return np.tile(idx.reshape(-1, 16).T, (8, 1)).astype(np.uint16)


def unstriped(offs):
    return offs[:16].T.reshape(-1).astype(np.int64)


E2M1 = np.array([0.0, 0.5, 1.0, 1.5, 2.0, 3.0, 4.0, 6.0, -0.0, -0.5, -1.0, -1.5, -2.0, -3.0, -4.0, -6.0])


def pack_weight(w, fmt):
    k, n = w.shape
    w = f64(np.asarray(w, np.float32).astype(ml_dtypes.bfloat16)).reshape(k // 32, 32, n)
    amax = np.abs(w).max(1)
    if fmt == "e4m3":
        byte = np.frexp(amax)[1] - 1 + 127 - 7
    else:
        mant, ex = np.frexp(amax / 6.0)
        byte = np.where(mant > 0.5, ex, ex - 1) + 127
    byte = np.clip(np.where(amax > 0, byte, 1), 1, 254)
    scaled = (w * np.exp2(127.0 - byte)[:, None, :]).reshape(k, n).astype(np.float32)
    by_word = np.ascontiguousarray(scaled.reshape(k // 512, 128, 4, n).transpose(0, 1, 3, 2))
    if fmt == "e4m3":
        words = by_word.astype(ml_dtypes.float8_e4m3fn).view(np.uint8)
    else:
        c = by_word.astype(ml_dtypes.float4_e2m1fn).view(np.uint8) & 0xF
        words = (c[..., 0::2] | (c[..., 1::2] << 4)).reshape(k // 512, 128, 2 * n)
    return np.ascontiguousarray(words), np.ascontiguousarray(byte.astype(np.uint8).reshape(k // 512, 16, n))


def unpack_weight(words, scales, fmt):
    g, _, n = scales.shape
    words = np.ascontiguousarray(words).reshape(g, 128, n, -1)
    if fmt == "e4m3":
        vals = words.view(ml_dtypes.float8_e4m3fn).astype(np.float64)
    else:
        nib = np.empty((g, 128, n, 4), np.uint8)
        nib[..., 0::2] = words & 0xF
        nib[..., 1::2] = words >> 4
        vals = E2M1[nib]
    vals = vals * np.repeat(np.exp2(scales.astype(np.float64) - 127.0), 8, axis=1)[..., None]
    return vals.transpose(0, 1, 3, 2).reshape(g * 512, n)


def gelu(v):
    return 0.5 * v * (1.0 + np.tanh(np.sqrt(2.0 / np.pi) * (v + 0.044715 * v**3)))


def bf(x):
    return np.asarray(x, np.float32).astype(ml_dtypes.bfloat16)


def planes(Y):
    n, m = Y.shape
    b = f64(bf(Y)).reshape(n // 32, 32, m)
    amax = np.abs(b).max(1)
    byte = np.clip(np.where(amax > 0, np.frexp(amax)[1] - 1 + 127 - 7, 1), 1, 254)
    codes = (b * np.exp2(127.0 - byte)[:, None, :]).reshape(n, m).astype(np.float32).astype(ml_dtypes.float8_e4m3fn).view(np.uint8)
    words = codes.reshape(n // 512, 128, 4, m).transpose(0, 1, 3, 2)
    return np.ascontiguousarray(words), np.ascontiguousarray(byte.astype(np.uint8).reshape(n // 512, 16, m))


K, H, N, T, S, T2, P = 512, 1024, 640, 4096, 1024, 2048, 1024

def setup_inputs():
    n = np.random.standard_normal
    s = mx_kscale(K)[:, None]
    u = mx_kscale(H)[:, None]
    d = {}
    d["tab_words"], d["tab_scales"] = pack_weight(n((K, T)) * s, "e4m3")
    d["offs"] = striped(np.random.permutation(T)[:S])
    d["offs2"] = striped(np.random.permutation(T2)[:S])
    d["offs3"] = striped(np.random.permutation(T2)[:P])
    d["w1"] = (0.8 * n((K, H)) / K**0.5 / s).astype(np.float32)
    d["w2_words"], d["w2_scales"] = pack_weight(n((K, H)) / K**0.5 / s, "e4m3")
    d["gain"] = (0.7 * np.exp(0.3 * n(H)) * u[:, 0]).astype(np.float32)
    d["page0"] = (n((H, T2)) * u).astype(np.float32)
    d["wgs"] = np.exp(0.3 * n((128, S))).astype(np.float32)
    d["bx"] = (0.5 * n(H) * u[:, 0]).astype(np.float32)
    d["w3_words"], d["w3_scales"] = pack_weight(1.2 * n((H, N)) / H**0.5 / u, "e2m1")
    d["w4"] = (n((H, N)) / H**0.5 / u).astype(np.float32)
    return d

def reference(tab_words, tab_scales, offs, offs2, offs3, w1, w2_words, w2_scales, gain, page0, wgs, bx, w3_words, w3_scales, w4):
    v = unpack_weight(tab_words, tab_scales, "e4m3")[:, unstriped(offs)]
    a = mxq(f64(w1), 0, "e4m3").T @ v
    b = unpack_weight(w2_words, w2_scales, "e4m3").T @ v
    h = f64(gain)[:, None] * (np.square(a) + b)
    page = f64(page0).copy()
    page[:, unstriped(offs2)] = np.tile(f64(wgs), (H // 128, 1)) * h
    x = page[:, unstriped(offs3)] + f64(bx)[:, None]
    xq = mxq(x, 0, "e4m3")
    c = unpack_weight(w3_words, w3_scales, "e2m1").T @ xq
    e = mxq(f64(w4), 0, "e4m3").T @ xq
    y = c + e * np.tanh(c)
    words, scales = planes(page)
    return y, page, words, scales

@@ -1,0 +1,321 @@
+from contextlib import ExitStack
+
+import concourse.mybir as mybir
+from concourse.masks import make_identity
+
+K, H, N, T, S, T2, PX = 512, 1024, 640, 4096, 1024, 2048, 1024
+FLOPS = 2 * (2 * K * H * S + 2 * H * N * PX)
+
+F32 = mybir.dt.float32
+BF16 = mybir.dt.bfloat16
+I32 = mybir.dt.int32
+U32 = mybir.dt.uint32
+U16 = mybir.dt.uint16
+U8 = mybir.dt.uint8
+FP8X4 = mybir.dt.float8_e4m3fn_x4
+FP4X4 = mybir.dt.float4_e2m1fn_x4
+ACT = mybir.ActivationFunctionType
+ALU = mybir.AluOpType
+
+P = 128
+BANK = 512
+HALF = 512
+GROUPS = H // 512
+TILES = 4
+
+
+def tile_list_aligner_stage_cells_kernel(
+    tc, tab_words, tab_scales, offs, offs2, offs3, w1, w2_words, w2_scales, gain, page0, wgs, bx,
+    w3_words, w3_scales, w4, out_0, out_1, out_2, out_3,
+):
+    nc = tc.nc
+    with ExitStack() as ctx:
+        keep = ctx.enter_context(tc.tile_pool(name="keep", bufs=1))
+        ring = ctx.enter_context(tc.tile_pool(name="ring", bufs=2))
+        psum = ctx.enter_context(tc.psum_pool(name="psum", bufs=4))
+
+        def words_of(dram_words):
+            return dram_words.rearrange("p c i -> p (c i)").bitcast(I32)
+
+        def load_scale_rows(queue, plane, rows):
+            for q in range(4):
+                queue.dma_start(out=plane[32 * q : 32 * q + 4].bitcast(I32), in_=rows[4 * q : 4 * q + 4].bitcast(I32))
+
+        list1 = keep.tile([P, S // 16], U16, name="list1")
+        list2 = keep.tile([P, S // 16], U16, name="list2")
+        list3 = keep.tile([P, PX // 16], U16, name="list3")
+        tabw = keep.tile([P, T], U32, name="tabw", align_bytes=64)
+        tabs = keep.tile([P, T], U8, name="tabs", align_bytes=64)
+        w2w = keep.tile([P, H], U32, name="w2w", align_bytes=64)
+        w2s = keep.tile([P, H], U8, name="w2s", align_bytes=64)
+        w3w = keep.tile([P, GROUPS, 2 * N], U8, name="w3w", align_bytes=64)
+        w3s = keep.tile([P, GROUPS, N], U8, name="w3s", align_bytes=64)
+        wgs_sb = keep.tile([P, S], F32, name="wgs_sb")
+        ident = keep.tile([P, P], F32, name="ident")
+        rows = keep.tile([P, P], F32, name="rows")
+        cols = keep.tile([P, 16], F32, name="cols")
+        warm = keep.tile([P, 1], F32, name="warm")
+
+        nc.vector.memset(tabs[:].bitcast(I32), 0)
+        nc.vector.memset(w2s[:].bitcast(I32), 0)
+        nc.vector.memset(rows[:], 0.0)
+        nc.vector.memset(w3s[:].rearrange("p a n -> p (a n)").bitcast(I32), 0)
+        nc.scalar.activation(out=warm[:], in_=rows[:, 0:1], func=ACT.Tanh)
+        make_identity(nc, ident[:])
+        nc.gpsimd.dma_start(out=rows[0:8, :], in_=gain.rearrange("(i p) -> i p", p=P))
+        nc.gpsimd.dma_start(out=rows[8:16, :], in_=bx.rearrange("(i p) -> i p", p=P))
+        load_scale_rows(nc.gpsimd, w3s, w3_scales.rearrange("a q n -> q a n"))
+
+        def load_raw(src, width):
+            raw = ring.tile([P, 4, width], F32, name="raw", tag="raw")
+            nc.sync.dma_start(out=raw[:], in_=src.rearrange("(p t) c -> p t c", t=4))
+            return raw
+
+        pages = {}
+
+        def load_page(i):
+            pages[i] = ring.tile([P, T2], F32, name="page", tag="page", bufs=5)
+            nc.sync.dma_start(out=pages[i][:], in_=page0[i * P : (i + 1) * P, :])
+
+        nc.sync.dma_start(out=tabw[:].bitcast(I32), in_=words_of(tab_words[0]))
+        load_scale_rows(nc.sync, tabs, tab_scales[0])
+        nc.sync.dma_start(out=list1[:], in_=offs)
+        w1_raw = [load_raw(w1[:, 0:512], 512)]
+        nc.sync.dma_start(out=w2w[:].bitcast(I32), in_=words_of(w2_words[0]))
+        load_scale_rows(nc.sync, w2s, w2_scales[0])
+        nc.sync.dma_start(out=list2[:], in_=offs2)
+        nc.sync.dma_start(out=wgs_sb[:], in_=wgs)
+        load_page(0)
+        load_page(1)
+        w1_raw.append(load_raw(w1[:, 512:1024], 512))
+        load_page(2)
+        load_page(3)
+        nc.sync.dma_start(out=list3[:], in_=offs3)
+        w4_raw = [load_raw(w4[512 * a : 512 * (a + 1), :], N) for a in range(GROUPS)]
+        nc.sync.dma_start(out=w3w[:].bitcast(I32), in_=w3_words.rearrange("a p c -> p a c").bitcast(I32))
+        load_page(4)
+
+        def interleave(copy, raw, width):
+            grouped = ring.tile([P, width, 4], BF16, name="grouped", tag="grouped", align_bytes=64)
+            copy(out=grouped[:].rearrange("p (c i) t -> p c t i", i=4), in_=raw[:].rearrange("p t (c i) -> p c t i", i=4))
+            return grouped[:].rearrange("p c t -> p (c t)")
+
+        def quantize(codes, scales, values):
+            nc.vector.quantize_mx(out=codes.bitcast(FP8X4), scales=scales, in_=values)
+
+        w1q = [keep.tile([P, 512], U32, name="w1q%d" % g, align_bytes=64) for g in range(GROUPS)]
+        w1s = [keep.tile([P, 512], U8, name="w1s%d" % g, align_bytes=64) for g in range(GROUPS)]
+        w4q = [keep.tile([P, N], U32, name="w4q%d" % g, align_bytes=64) for g in range(GROUPS)]
+        w4s = [keep.tile([P, N], U8, name="w4s%d" % g, align_bytes=64) for g in range(GROUPS)]
+        vq = [keep.tile([P, HALF], U32, name="vq%d" % hf, align_bytes=64) for hf in range(2)]
+        vs = [keep.tile([P, HALF], U8, name="vs%d" % hf, align_bytes=64) for hf in range(2)]
+        xq = {(g, hf): keep.tile([P, HALF], U32, name="xq%d%d" % (g, hf), align_bytes=64) for g in range(GROUPS) for hf in range(2)}
+        xs = {(g, hf): keep.tile([P, HALF], U8, name="xs%d%d" % (g, hf), align_bytes=64) for g in range(GROUPS) for hf in range(2)}
+
+        def half_of(lst, hf):
+            return lst[:, hf * (HALF // 16) : (hf + 1) * (HALF // 16)]
+
+        def prepare_w1(g, copy):
+            quantize(w1q[g][:], w1s[g][:], interleave(copy, w1_raw[g], 512))
+
+        def prepare_w4(g):
+            values = interleave(nc.scalar.copy, w4_raw[g], N)
+            quantize(w4q[g][:, 0:512], w4s[g][:, 0:512], values[:, 0:2048])
+            quantize(w4q[g][:, 512:N], w4s[g][:, 512:N], values[:, 2048 : 4 * N])
+
+        def gather_table(hf):
+            nc.vector.tensor_copy(out=vq[hf][:], in_=tabw[:].indirect(half_of(list1, hf)))
+            nc.vector.tensor_copy(out=vs[hf][:], in_=tabs[:].indirect(half_of(list1, hf)))
+
+        def bank(tag):
+            return psum.tile([P, BANK], F32, name=tag, tag=tag)
+
+        def add_transposed(out, first, second):
+            nc.tensor.matmul(out, lhsT=first, rhs=ident[:], is_transpose=True, start=True, stop=False)
+            nc.tensor.matmul(out, lhsT=second, rhs=ident[:], is_transpose=True, start=False, stop=True)
+
+        sq, bt, h = {}, {}, {}
+
+        def products(g, hf, jb, copy):
+            cj = slice(jb * P, (jb + 1) * P)
+            cr = slice(g * 512, (g + 1) * 512)
+            a_ps, b_ps = bank("mm"), bank("mm")
+            nc.tensor.matmul_mx(out=a_ps[:], lhsT=vq[hf][:, cj].bitcast(FP8X4), lhsT_scale=vs[hf][:, cj],
+                                rhs=w1q[g][:].bitcast(FP8X4), rhs_scale=w1s[g][:], start=True, stop=True)
+            nc.tensor.matmul_mx(out=b_ps[:], lhsT=vq[hf][:, cj].bitcast(FP8X4), lhsT_scale=vs[hf][:, cj],
+                                rhs=w2w[:, cr].bitcast(FP8X4), rhs_scale=w2s[:, cr], start=True, stop=True)
+            sq[jb] = ring.tile([P, BANK], F32, name="sq", tag="sq", bufs=4)
+            bt[jb] = ring.tile([P, BANK], F32, name="bt", tag="bt", bufs=4)
+            nc.scalar.activation(out=sq[jb][:], in_=a_ps[:], func=ACT.Square)
+            copy(out=bt[jb][:], in_=b_ps[:])
+
+        def make_h(g, hf, i):
+            h_ps = bank("tr")
+            cr = slice(i * P, (i + 1) * P)
+            for jb in range(4):
+                add_transposed(h_ps[:, jb * P : (jb + 1) * P], sq[jb][:, cr], bt[jb][:, cr])
+            h[g, hf, i] = ring.tile([P, HALF], F32, name="h", tag="h", bufs=8)
+            tile_no = TILES * g + i
+            nc.scalar.activation(out=h[g, hf, i][:], in_=h_ps[:], func=ACT.Copy, scale=cols[:, tile_no : tile_no + 1])
+
+        def produce(g, hf, copy):
+            for jb in range(4):
+                products(g, hf, jb, copy)
+            for i in range(TILES):
+                make_h(g, hf, i)
+
+        def scatter(g, hf, i):
+            nc.vector.tensor_tensor(out=pages[TILES * g + i][:].indirect(half_of(list2, hf)), in0=h[g, hf, i][:],
+                                    in1=wgs_sb[:, hf * HALF : (hf + 1) * HALF], op=ALU.mult)
+
+        def round_sorted(turned, i, turned_ps):
+            nc.scalar.copy(
+                out=turned[:].rearrange("m b (u p e) -> m b u p e", u=2, e=2)[:, :, :, 32 * i : 32 * (i + 1), :],
+                in_=turned_ps[:].rearrange("m (b p u e) -> m b u p e", b=4, u=2, e=2),
+            )
+
+        def turn_back(turned):
+            words = turned[:].rearrange("m b r -> m (b r)").bitcast(F32)
+            woven = ring.tile([P, 4 * BANK], BF16, name="woven", tag="woven", bufs=6, align_bytes=64)
+            woven_words = woven[:].bitcast(F32)
+            for pair in range(2):
+                back_ps = bank("tr")
+                for s in range(4):
+                    src = (4 * pair + s) * P
+                    nc.tensor.transpose(back_ps[:, s * P : (s + 1) * P], words[:, src : src + P], ident[:])
+                nc.scalar.copy(
+                    out=woven_words[:, pair * BANK : (pair + 1) * BANK].rearrange("p (b m u) -> p b m u", b=2, u=2),
+                    in_=back_ps[:].rearrange("p (b u m) -> p b m u", b=2, u=2),
+                )
+            return woven
+
+        x_turned, page_turned, picked = {}, {}, {}
+
+        def pick(g, hf, i):
+            picked[hf] = ring.tile([P, HALF], F32, name="picked", tag="picked", bufs=8)
+            nc.vector.tensor_copy(out=picked[hf][:], in_=pages[TILES * g + i][:].indirect(half_of(list3, hf)))
+
+        def turn_x(g, hf, i):
+            if i == 0:
+                x_turned[hf] = ring.tile([P, 4, 512], BF16, name="x_turned", tag="x_turned")
+            x_ps = bank("tr")
+            col = 8 + TILES * g + i
+            for jb in range(4):
+                nc.tensor.matmul(x_ps[:, jb * P : (jb + 1) * P], lhsT=cols[:, col : col + 1].to_broadcast([P, P]),
+                                 rhs=ident[:], is_transpose=True, start=(jb == 0), stop=False)
+            for jb in range(4):
+                nc.tensor.matmul(x_ps[:, jb * P : (jb + 1) * P], lhsT=picked[hf][:, jb * P : (jb + 1) * P],
+                                 rhs=ident[:], is_transpose=True, start=False, stop=(jb == 3))
+            round_sorted(x_turned[hf], i, x_ps)
+
+        def turn_page(g, i, quarter):
+            if i == 0:
+                page_turned[quarter] = ring.tile([P, 4, 512], BF16, name="page_turned", tag="page_turned", bufs=4)
+            page_ps = bank("tr")
+            for b in range(4):
+                src = (4 * quarter + b) * P
+                nc.tensor.transpose(page_ps[:, b * P : (b + 1) * P], pages[TILES * g + i][:, src : src + P], ident[:])
+            round_sorted(page_turned[quarter], i, page_ps)
+
+        def store_page(tile_no):
+            nc.sync.dma_start(out=out_1[tile_no * P : (tile_no + 1) * P, :], in_=pages[tile_no][:])
+
+        def finish_x(g, hf):
+            quantize(xq[g, hf][:], xs[g, hf][:], turn_back(x_turned[hf])[:])
+
+        plane_words, plane_scales = {}, {}
+
+        def finish_page(g, quarter):
+            if quarter == 0:
+                plane_words[g] = ring.tile([P, T2], U32, name="plane_words", tag="plane_words", bufs=1, align_bytes=64)
+                plane_scales[g] = ring.tile([P, T2], U8, name="plane_scales", tag="plane_scales", bufs=1, align_bytes=64)
+            cm = slice(quarter * 512, (quarter + 1) * 512)
+            quantize(plane_words[g][:, cm], plane_scales[g][:, cm], turn_back(page_turned[quarter])[:])
+            nc.sync.dma_start(out=words_of(out_2[g])[:, cm], in_=plane_words[g][:, cm].bitcast(I32))
+            if quarter == 3:
+                for q in range(4):
+                    nc.sync.dma_start(out=out_3[g, 4 * q : 4 * q + 4, :].bitcast(I32),
+                                      in_=plane_scales[g][32 * q : 32 * q + 4, :].bitcast(I32))
+
+        second = {}
+
+        def second_products(hf, nt):
+            c_ps, e_ps = bank("mm"), bank("tr")
+            cn = slice(nt * P, (nt + 1) * P)
+            for g in range(GROUPS):
+                nc.tensor.matmul_mx(out=c_ps[:], lhsT=w3w[:, g, 2 * nt * P : 2 * (nt + 1) * P].bitcast(FP4X4),
+                                    lhsT_scale=w3s[:, g, cn], rhs=xq[g, hf][:].bitcast(FP8X4), rhs_scale=xs[g, hf][:],
+                                    start=(g == 0), stop=(g == GROUPS - 1))
+            for g in range(GROUPS):
+                nc.tensor.matmul_mx(out=e_ps[:], lhsT=w4q[g][:, cn].bitcast(FP8X4), lhsT_scale=w4s[g][:, cn],
+                                    rhs=xq[g, hf][:].bitcast(FP8X4), rhs_scale=xs[g, hf][:],
+                                    start=(g == 0), stop=(g == GROUPS - 1))
+            th = ring.tile([P, BANK], F32, name="th", tag="sq", bufs=4)
+            nc.scalar.activation(out=th[:], in_=c_ps[:], func=ACT.Tanh)
+            gated = ring.tile([P, BANK], F32, name="gated", tag="bt", bufs=4)
+            nc.vector.tensor_tensor(out=gated[:], in0=e_ps[:], in1=th[:], op=ALU.mult)
+            second[hf, nt] = (c_ps, gated)
+
+        def second_sum(hf, nt):
+            c_ps, gated = second[hf, nt]
+            y = ring.tile([P, BANK], F32, name="y", tag="h", bufs=8)
+            nc.vector.tensor_tensor(out=y[:], in0=c_ps[:], in1=gated[:], op=ALU.add)
+            nc.sync.dma_start(out=out_0[nt * P : (nt + 1) * P, hf * HALF : (hf + 1) * HALF], in_=y[:])
+
+        cols_ps = bank("tr")
+        nc.tensor.transpose(cols_ps[:, 0:P], rows[:], ident[:])
+        nc.scalar.copy(out=cols[:], in_=cols_ps[:, 0:16])
+
+        gather_table(0)
+        prepare_w1(0, nc.vector.tensor_copy)
+        produce(0, 0, nc.vector.tensor_copy)
+        gather_table(1)
+        produce(0, 1, nc.scalar.copy)
+        prepare_w1(1, nc.scalar.copy)
+        for i in range(TILES):
+            scatter(0, 0, i)
+        produce(1, 0, nc.scalar.copy)
+        for i in range(TILES):
+            scatter(0, 1, i)
+            store_page(i)
+            for hf in range(2):
+                pick(0, hf, i)
+            for hf in range(2):
+                turn_x(0, hf, i)
+            for quarter in range(4):
+                turn_page(0, i, quarter)
+            if i < 3:
+                load_page(5 + i)
+            products(1, 1, i, nc.scalar.copy)
+            if i < GROUPS:
+                prepare_w4(i)
+        for i in range(TILES):
+            scatter(1, 0, i)
+        for hf in range(2):
+            finish_x(0, hf)
+        for quarter in range(4):
+            finish_page(0, quarter)
+        for i in range(TILES):
+            make_h(1, 1, i)
+        for i in range(TILES):
+            scatter(1, 1, i)
+            store_page(TILES + i)
+            for hf in range(2):
+                pick(1, hf, i)
+            for hf in range(2):
+                turn_x(1, hf, i)
+                if i == TILES - 1:
+                    finish_x(1, hf)
+            if i < TILES - 1:
+                for quarter in range(4):
+                    turn_page(1, i, quarter)
+        steps = [(hf, nt) for hf in range(2) for nt in range(N // P)]
+        for s, (hf, nt) in enumerate(steps):
+            second_products(hf, nt)
+            if s > 0:
+                second_sum(*steps[s - 1])
+            if s < 4:
+                turn_page(1, TILES - 1, s)
+            if 1 <= s < 5:
+                finish_page(1, s - 1)
+        second_sum(*steps[-1])

@@ -22,6 +22,12 @@ BANK = 512
 HALF = 512
 GROUPS = H // 512
 TILES = 4
+PAGE_BUFS = 5
+RAW_AT = PAGE_BUFS * T2 * 4
+W2_AT = RAW_AT + 2 * 4 * N * 4
+WGS_AT = W2_AT + H * 4
+W3_AT = WGS_AT + S * 4
+LATE_BYTES = W3_AT + GROUPS * 2 * N
 
 
 def tile_list_aligner_stage_cells_kernel(
@@ -32,7 +38,8 @@ def tile_list_aligner_stage_cells_kernel(
     with ExitStack() as ctx:
         keep = ctx.enter_context(tc.tile_pool(name="keep", bufs=1))
         ring = ctx.enter_context(tc.tile_pool(name="ring", bufs=2))
-        psum = ctx.enter_context(tc.psum_pool(name="psum", bufs=4))
+        late = ctx.enter_context(tc.tile_pool(name="late", bufs=1))
+        psum = ctx.enter_context(tc.psum_pool(name="psum", bufs=8))
 
         def words_of(dram_words):
             return dram_words.rearrange("p c i -> p (c i)").bitcast(I32)
@@ -46,59 +53,63 @@ def tile_list_aligner_stage_cells_kernel(
         list3 = keep.tile([P, PX // 16], U16, name="list3")
         tabw = keep.tile([P, T], U32, name="tabw", align_bytes=64)
         tabs = keep.tile([P, T], U8, name="tabs", align_bytes=64)
-        w2w = keep.tile([P, H], U32, name="w2w", align_bytes=64)
         w2s = keep.tile([P, H], U8, name="w2s", align_bytes=64)
-        w3w = keep.tile([P, GROUPS, 2 * N], U8, name="w3w", align_bytes=64)
         w3s = keep.tile([P, GROUPS, N], U8, name="w3s", align_bytes=64)
-        wgs_sb = keep.tile([P, S], F32, name="wgs_sb")
         ident = keep.tile([P, P], F32, name="ident")
-        rows = keep.tile([P, P], F32, name="rows")
-        cols = keep.tile([P, 16], F32, name="cols")
-        warm = keep.tile([P, 1], F32, name="warm")
+        gain_rows = keep.tile([P, P], F32, name="gain_rows")
+        bx_rows = keep.tile([P, P], F32, name="bx_rows")
+        gain_cols = keep.tile([P, 8], F32, name="gain_cols")
+        bx_cols = keep.tile([P, 8], F32, name="bx_cols")
+        warm = late.tile([P, LATE_BYTES // 4], F32, name="warm", offset=0)
+        w2w = late.tile([P, H], U32, name="w2w", align_bytes=64, offset=W2_AT)
+        wgs_sb = late.tile([P, S], F32, name="wgs_sb", offset=WGS_AT)
+        w3w = late.tile([P, GROUPS, 2 * N], U8, name="w3w", align_bytes=64, offset=W3_AT)
 
-        nc.vector.memset(tabs[:].bitcast(I32), 0)
         nc.vector.memset(w2s[:].bitcast(I32), 0)
-        nc.vector.memset(rows[:], 0.0)
+        nc.vector.memset(bx_rows[:], 0.0)
+        nc.vector.memset(tabs[:].bitcast(I32), 0)
+        nc.vector.memset(gain_rows[:], 0.0)
         nc.vector.memset(w3s[:].rearrange("p a n -> p (a n)").bitcast(I32), 0)
-        nc.scalar.activation(out=warm[:], in_=rows[:, 0:1], func=ACT.Tanh)
+        nc.scalar.activation(out=warm[:, 0:1], in_=gain_rows[:, 0:1], func=ACT.Tanh)
+        load_scale_rows(nc.gpsimd, w2s, w2_scales[0])
         make_identity(nc, ident[:])
-        nc.gpsimd.dma_start(out=rows[0:8, :], in_=gain.rearrange("(i p) -> i p", p=P))
-        nc.gpsimd.dma_start(out=rows[8:16, :], in_=bx.rearrange("(i p) -> i p", p=P))
+        nc.gpsimd.dma_start(out=bx_rows[0:8, :], in_=bx.rearrange("(i p) -> i p", p=P))
         load_scale_rows(nc.gpsimd, w3s, w3_scales.rearrange("a q n -> q a n"))
 
         def load_raw(src, width):
-            raw = ring.tile([P, 4, width], F32, name="raw", tag="raw")
+            raw = late.tile([P, 4, width], F32, name="raw", tag="raw", bufs=2, offset=RAW_AT)
             nc.sync.dma_start(out=raw[:], in_=src.rearrange("(p t) c -> p t c", t=4))
             return raw
 
         pages = {}
 
         def load_page(i):
-            pages[i] = ring.tile([P, T2], F32, name="page", tag="page", bufs=5)
+            pages[i] = late.tile([P, T2], F32, name="page", tag="page", bufs=PAGE_BUFS, offset=0)
             nc.sync.dma_start(out=pages[i][:], in_=page0[i * P : (i + 1) * P, :])
 
+        nc.sync.dma_start(out=list1[:], in_=offs)
+        nc.sync.dma_start(out=list2[:], in_=offs2)
+        nc.sync.dma_start(out=list3[:], in_=offs3)
         nc.sync.dma_start(out=tabw[:].bitcast(I32), in_=words_of(tab_words[0]))
         load_scale_rows(nc.sync, tabs, tab_scales[0])
-        nc.sync.dma_start(out=list1[:], in_=offs)
+        nc.sync.dma_start(out=gain_rows[0:8, :], in_=gain.rearrange("(i p) -> i p", p=P))
         w1_raw = [load_raw(w1[:, 0:512], 512)]
         nc.sync.dma_start(out=w2w[:].bitcast(I32), in_=words_of(w2_words[0]))
-        load_scale_rows(nc.sync, w2s, w2_scales[0])
-        nc.sync.dma_start(out=list2[:], in_=offs2)
         nc.sync.dma_start(out=wgs_sb[:], in_=wgs)
         load_page(0)
         load_page(1)
         w1_raw.append(load_raw(w1[:, 512:1024], 512))
-        load_page(2)
-        load_page(3)
-        nc.sync.dma_start(out=list3[:], in_=offs3)
-        w4_raw = [load_raw(w4[512 * a : 512 * (a + 1), :], N) for a in range(GROUPS)]
+        for i in range(2, PAGE_BUFS):
+            load_page(i)
         nc.sync.dma_start(out=w3w[:].bitcast(I32), in_=w3_words.rearrange("a p c -> p a c").bitcast(I32))
-        load_page(4)
+        w4_raw = {a: load_raw(w4[512 * a : 512 * (a + 1), :], N) for a in reversed(range(GROUPS))}
 
-        def interleave(copy, raw, width):
-            grouped = ring.tile([P, width, 4], BF16, name="grouped", tag="grouped", align_bytes=64)
-            copy(out=grouped[:].rearrange("p (c i) t -> p c t i", i=4), in_=raw[:].rearrange("p t (c i) -> p c t i", i=4))
-            return grouped[:].rearrange("p c t -> p (c t)")
+        def interleave(raw, width, piece):
+            grouped = ring.tile([P, 4 * width], BF16, name="grouped", tag="grouped", align_bytes=64)
+            for c in range(0, width, piece):
+                nc.scalar.copy(out=grouped[:, 4 * c : 4 * (c + piece)].rearrange("p (c i t) -> p c t i", i=4, t=4),
+                               in_=raw[:, :, c : c + piece].rearrange("p t (c i) -> p c t i", i=4))
+            return grouped[:]
 
         def quantize(codes, scales, values):
             nc.vector.quantize_mx(out=codes.bitcast(FP8X4), scales=scales, in_=values)
@@ -115,11 +126,11 @@ def tile_list_aligner_stage_cells_kernel(
         def half_of(lst, hf):
             return lst[:, hf * (HALF // 16) : (hf + 1) * (HALF // 16)]
 
-        def prepare_w1(g, copy):
-            quantize(w1q[g][:], w1s[g][:], interleave(copy, w1_raw[g], 512))
+        def prepare_w1(g):
+            quantize(w1q[g][:], w1s[g][:], interleave(w1_raw[g], 512, P))
 
         def prepare_w4(g):
-            values = interleave(nc.scalar.copy, w4_raw[g], N)
+            values = interleave(w4_raw[g], N, P)
             quantize(w4q[g][:, 0:512], w4s[g][:, 0:512], values[:, 0:2048])
             quantize(w4q[g][:, 512:N], w4s[g][:, 512:N], values[:, 2048 : 4 * N])
 
@@ -128,7 +139,7 @@ def tile_list_aligner_stage_cells_kernel(
             nc.vector.tensor_copy(out=vs[hf][:], in_=tabs[:].indirect(half_of(list1, hf)))
 
         def bank(tag):
-            return psum.tile([P, BANK], F32, name=tag, tag=tag)
+            return psum.tile([P, BANK], F32, name="bank", tag="bank")
 
         def add_transposed(out, first, second):
             nc.tensor.matmul(out, lhsT=first, rhs=ident[:], is_transpose=True, start=True, stop=False)
@@ -156,7 +167,7 @@ def tile_list_aligner_stage_cells_kernel(
                 add_transposed(h_ps[:, jb * P : (jb + 1) * P], sq[jb][:, cr], bt[jb][:, cr])
             h[g, hf, i] = ring.tile([P, HALF], F32, name="h", tag="h", bufs=8)
             tile_no = TILES * g + i
-            nc.scalar.activation(out=h[g, hf, i][:], in_=h_ps[:], func=ACT.Copy, scale=cols[:, tile_no : tile_no + 1])
+            nc.scalar.activation(out=h[g, hf, i][:], in_=h_ps[:], func=ACT.Copy, scale=gain_cols[:, tile_no : tile_no + 1])
 
         def produce(g, hf, copy):
             for jb in range(4):
@@ -168,13 +179,13 @@ def tile_list_aligner_stage_cells_kernel(
             nc.vector.tensor_tensor(out=pages[TILES * g + i][:].indirect(half_of(list2, hf)), in0=h[g, hf, i][:],
                                     in1=wgs_sb[:, hf * HALF : (hf + 1) * HALF], op=ALU.mult)
 
-        def round_sorted(turned, i, turned_ps):
-            nc.scalar.copy(
+        def round_sorted(copy, turned, i, turned_ps):
+            copy(
                 out=turned[:].rearrange("m b (u p e) -> m b u p e", u=2, e=2)[:, :, :, 32 * i : 32 * (i + 1), :],
                 in_=turned_ps[:].rearrange("m (b p u e) -> m b u p e", b=4, u=2, e=2),
             )
 
-        def turn_back(turned):
+        def turn_back(turned, copies):
             words = turned[:].rearrange("m b r -> m (b r)").bitcast(F32)
             woven = ring.tile([P, 4 * BANK], BF16, name="woven", tag="woven", bufs=6, align_bytes=64)
             woven_words = woven[:].bitcast(F32)
@@ -183,7 +194,7 @@ def tile_list_aligner_stage_cells_kernel(
                 for s in range(4):
                     src = (4 * pair + s) * P
                     nc.tensor.transpose(back_ps[:, s * P : (s + 1) * P], words[:, src : src + P], ident[:])
-                nc.scalar.copy(
+                copies[pair](
                     out=woven_words[:, pair * BANK : (pair + 1) * BANK].rearrange("p (b m u) -> p b m u", b=2, u=2),
                     in_=back_ps[:].rearrange("p (b u m) -> p b m u", b=2, u=2),
                 )
@@ -192,21 +203,21 @@ def tile_list_aligner_stage_cells_kernel(
         x_turned, page_turned, picked = {}, {}, {}
 
         def pick(g, hf, i):
-            picked[hf] = ring.tile([P, HALF], F32, name="picked", tag="picked", bufs=8)
-            nc.vector.tensor_copy(out=picked[hf][:], in_=pages[TILES * g + i][:].indirect(half_of(list3, hf)))
+            picked[i, hf] = ring.tile([P, HALF], F32, name="picked", tag="picked", bufs=8)
+            nc.vector.tensor_copy(out=picked[i, hf][:], in_=pages[TILES * g + i][:].indirect(half_of(list3, hf)))
 
-        def turn_x(g, hf, i):
+        def turn_x(g, hf, i, copy):
             if i == 0:
                 x_turned[hf] = ring.tile([P, 4, 512], BF16, name="x_turned", tag="x_turned")
             x_ps = bank("tr")
-            col = 8 + TILES * g + i
+            col = TILES * g + i
             for jb in range(4):
-                nc.tensor.matmul(x_ps[:, jb * P : (jb + 1) * P], lhsT=cols[:, col : col + 1].to_broadcast([P, P]),
+                nc.tensor.matmul(x_ps[:, jb * P : (jb + 1) * P], lhsT=bx_cols[:, col : col + 1].to_broadcast([P, P]),
                                  rhs=ident[:], is_transpose=True, start=(jb == 0), stop=False)
             for jb in range(4):
-                nc.tensor.matmul(x_ps[:, jb * P : (jb + 1) * P], lhsT=picked[hf][:, jb * P : (jb + 1) * P],
+                nc.tensor.matmul(x_ps[:, jb * P : (jb + 1) * P], lhsT=picked[i, hf][:, jb * P : (jb + 1) * P],
                                  rhs=ident[:], is_transpose=True, start=False, stop=(jb == 3))
-            round_sorted(x_turned[hf], i, x_ps)
+            round_sorted(copy, x_turned[hf], i, x_ps)
 
         def turn_page(g, i, quarter):
             if i == 0:
@@ -215,13 +226,13 @@ def tile_list_aligner_stage_cells_kernel(
             for b in range(4):
                 src = (4 * quarter + b) * P
                 nc.tensor.transpose(page_ps[:, b * P : (b + 1) * P], pages[TILES * g + i][:, src : src + P], ident[:])
-            round_sorted(page_turned[quarter], i, page_ps)
+            round_sorted(nc.scalar.copy, page_turned[quarter], i, page_ps)
 
         def store_page(tile_no):
             nc.sync.dma_start(out=out_1[tile_no * P : (tile_no + 1) * P, :], in_=pages[tile_no][:])
 
-        def finish_x(g, hf):
-            quantize(xq[g, hf][:], xs[g, hf][:], turn_back(x_turned[hf])[:])
+        def finish_x(g, hf, copies):
+            quantize(xq[g, hf][:], xs[g, hf][:], turn_back(x_turned[hf], copies)[:])
 
         plane_words, plane_scales = {}, {}
 
@@ -230,7 +241,7 @@ def tile_list_aligner_stage_cells_kernel(
                 plane_words[g] = ring.tile([P, T2], U32, name="plane_words", tag="plane_words", bufs=1, align_bytes=64)
                 plane_scales[g] = ring.tile([P, T2], U8, name="plane_scales", tag="plane_scales", bufs=1, align_bytes=64)
             cm = slice(quarter * 512, (quarter + 1) * 512)
-            quantize(plane_words[g][:, cm], plane_scales[g][:, cm], turn_back(page_turned[quarter])[:])
+            quantize(plane_words[g][:, cm], plane_scales[g][:, cm], turn_back(page_turned[quarter], on_scalar)[:])
             nc.sync.dma_start(out=words_of(out_2[g])[:, cm], in_=plane_words[g][:, cm].bitcast(I32))
             if quarter == 3:
                 for q in range(4):
@@ -242,14 +253,14 @@ def tile_list_aligner_stage_cells_kernel(
         def second_products(hf, nt):
             c_ps, e_ps = bank("mm"), bank("tr")
             cn = slice(nt * P, (nt + 1) * P)
-            for g in range(GROUPS):
+            for g in reversed(range(GROUPS)):
                 nc.tensor.matmul_mx(out=c_ps[:], lhsT=w3w[:, g, 2 * nt * P : 2 * (nt + 1) * P].bitcast(FP4X4),
                                     lhsT_scale=w3s[:, g, cn], rhs=xq[g, hf][:].bitcast(FP8X4), rhs_scale=xs[g, hf][:],
-                                    start=(g == 0), stop=(g == GROUPS - 1))
-            for g in range(GROUPS):
+                                    start=(g == GROUPS - 1), stop=(g == 0))
+            for g in reversed(range(GROUPS)):
                 nc.tensor.matmul_mx(out=e_ps[:], lhsT=w4q[g][:, cn].bitcast(FP8X4), lhsT_scale=w4s[g][:, cn],
                                     rhs=xq[g, hf][:].bitcast(FP8X4), rhs_scale=xs[g, hf][:],
-                                    start=(g == 0), stop=(g == GROUPS - 1))
+                                    start=(g == GROUPS - 1), stop=(g == 0))
             th = ring.tile([P, BANK], F32, name="th", tag="sq", bufs=4)
             nc.scalar.activation(out=th[:], in_=c_ps[:], func=ACT.Tanh)
             gated = ring.tile([P, BANK], F32, name="gated", tag="bt", bufs=4)
@@ -262,60 +273,83 @@ def tile_list_aligner_stage_cells_kernel(
             nc.vector.tensor_tensor(out=y[:], in0=c_ps[:], in1=gated[:], op=ALU.add)
             nc.sync.dma_start(out=out_0[nt * P : (nt + 1) * P, hf * HALF : (hf + 1) * HALF], in_=y[:])
 
-        cols_ps = bank("tr")
-        nc.tensor.transpose(cols_ps[:, 0:P], rows[:], ident[:])
-        nc.scalar.copy(out=cols[:], in_=cols_ps[:, 0:16])
+        on_scalar = (nc.scalar.copy, nc.scalar.copy)
+
+        def to_columns(cols, rows):
+            cols_ps = bank("tr")
+            nc.tensor.transpose(cols_ps[:, 0:P], rows[:], ident[:])
+            nc.scalar.copy(out=cols[:], in_=cols_ps[:, 0:8])
+
+        def picks(g, i):
+            for hf in range(2):
+                pick(g, hf, i)
+
+        def turns(g, i):
+            for hf in range(2):
+                turn_x(g, hf, i, nc.scalar.copy)
+
+        def page_turns(g, i):
+            for quarter in range(4):
+                turn_page(g, i, quarter)
 
         gather_table(0)
-        prepare_w1(0, nc.vector.tensor_copy)
-        produce(0, 0, nc.vector.tensor_copy)
         gather_table(1)
+        prepare_w1(0)
+        to_columns(gain_cols, gain_rows)
+        produce(0, 0, nc.vector.tensor_copy)
+        prepare_w1(1)
         produce(0, 1, nc.scalar.copy)
-        prepare_w1(1, nc.scalar.copy)
+        to_columns(bx_cols, bx_rows)
         for i in range(TILES):
             scatter(0, 0, i)
         produce(1, 0, nc.scalar.copy)
-        for i in range(TILES):
-            scatter(0, 1, i)
-            store_page(i)
-            for hf in range(2):
-                pick(0, hf, i)
-            for hf in range(2):
-                turn_x(0, hf, i)
-            for quarter in range(4):
-                turn_page(0, i, quarter)
-            if i < 3:
-                load_page(5 + i)
-            products(1, 1, i, nc.scalar.copy)
-            if i < GROUPS:
-                prepare_w4(i)
+        for jb in range(4):
+            products(1, 1, jb, nc.scalar.copy)
+        last = TILES - 1
+
+        def second_half(g):
+            for i in range(TILES):
+                if i == last:
+                    picks(g, i - 1)
+                    turns(g, i - 1)
+                scatter(g, 1, i)
+                store_page(TILES * g + i)
+                if 0 < i < last:
+                    picks(g, i - 1)
+                    turns(g, i - 1)
+                if g == 0 or i < last:
+                    page_turns(g, i)
+                if g == 0 and i > 0:
+                    load_page(TILES + i)
+            picks(g, last)
+
+        second_half(0)
+        turns(0, last)
         for i in range(TILES):
             scatter(1, 0, i)
         for hf in range(2):
-            finish_x(0, hf)
+            finish_x(0, hf, on_scalar)
         for quarter in range(4):
             finish_page(0, quarter)
         for i in range(TILES):
             make_h(1, 1, i)
-        for i in range(TILES):
-            scatter(1, 1, i)
-            store_page(TILES + i)
-            for hf in range(2):
-                pick(1, hf, i)
-            for hf in range(2):
-                turn_x(1, hf, i)
-                if i == TILES - 1:
-                    finish_x(1, hf)
-            if i < TILES - 1:
-                for quarter in range(4):
-                    turn_page(1, i, quarter)
+        for g in reversed(range(GROUPS)):
+            prepare_w4(g)
+        second_half(1)
+        for quarter in range(2):
+            turn_page(1, last, quarter)
+        turn_x(1, 0, last, nc.scalar.copy)
+        turn_page(1, last, 2)
+        turn_x(1, 1, last, nc.vector.tensor_copy)
+        finish_x(1, 0, (nc.scalar.copy, nc.vector.tensor_copy))
+        turn_page(1, last, 3)
+        finish_x(1, 1, (nc.scalar.copy, nc.vector.tensor_copy))
+        finish_page(1, 0)
         steps = [(hf, nt) for hf in range(2) for nt in range(N // P)]
         for s, (hf, nt) in enumerate(steps):
             second_products(hf, nt)
             if s > 0:
                 second_sum(*steps[s - 1])
-            if s < 4:
-                turn_page(1, TILES - 1, s)
-            if 1 <= s < 5:
-                finish_page(1, s - 1)
+            if s in (1, 3, 5):
+                finish_page(1, (s + 1) // 2)
         second_sum(*steps[-1])

@@ -18,16 +18,24 @@ ACT = mybir.ActivationFunctionType
 ALU = mybir.AluOpType
 
 P = 128
+PASS = 512
 BANK = 512
 HALF = 512
-GROUPS = H // 512
-TILES = 4
+BLOCKS = BANK // P
+GROUPS = H // PASS
+TILES = PASS // P
+QUARTERS = T2 // BANK
+
+PAGE_BYTES = T2 * 4
 PAGE_BUFS = 5
-RAW_AT = PAGE_BUFS * T2 * 4
-W2_AT = RAW_AT + 2 * 4 * N * 4
-WGS_AT = W2_AT + H * 4
+RAW_AT = PAGE_BUFS * PAGE_BYTES
+RAW_BYTES = 4 * N * 4
+W2_AT = RAW_AT + 2 * RAW_BYTES
+W2S_AT = W2_AT + H * 4
+WGS_AT = W2S_AT + H
 W3_AT = WGS_AT + S * 4
-LATE_BYTES = W3_AT + GROUPS * 2 * N
+TAB_AT = W3_AT + GROUPS * 2 * N
+V1_AT = TAB_AT + T * 4
 
 
 def tile_list_aligner_stage_cells_kernel(
@@ -38,7 +46,7 @@ def tile_list_aligner_stage_cells_kernel(
     with ExitStack() as ctx:
         keep = ctx.enter_context(tc.tile_pool(name="keep", bufs=1))
         ring = ctx.enter_context(tc.tile_pool(name="ring", bufs=2))
-        late = ctx.enter_context(tc.tile_pool(name="late", bufs=1))
+        placed = ctx.enter_context(tc.tile_pool(name="placed", bufs=1))
         psum = ctx.enter_context(tc.psum_pool(name="psum", bufs=8))
 
         def words_of(dram_words):
@@ -51,305 +59,364 @@ def tile_list_aligner_stage_cells_kernel(
         list1 = keep.tile([P, S // 16], U16, name="list1")
         list2 = keep.tile([P, S // 16], U16, name="list2")
         list3 = keep.tile([P, PX // 16], U16, name="list3")
-        tabw = keep.tile([P, T], U32, name="tabw", align_bytes=64)
+        tabw = placed.tile([P, T], U32, name="tabw", align_bytes=64, offset=TAB_AT)
         tabs = keep.tile([P, T], U8, name="tabs", align_bytes=64)
-        w2s = keep.tile([P, H], U8, name="w2s", align_bytes=64)
         w3s = keep.tile([P, GROUPS, N], U8, name="w3s", align_bytes=64)
         ident = keep.tile([P, P], F32, name="ident")
         gain_rows = keep.tile([P, P], F32, name="gain_rows")
         bx_rows = keep.tile([P, P], F32, name="bx_rows")
-        gain_cols = keep.tile([P, 8], F32, name="gain_cols")
-        bx_cols = keep.tile([P, 8], F32, name="bx_cols")
-        warm = late.tile([P, LATE_BYTES // 4], F32, name="warm", offset=0)
-        w2w = late.tile([P, H], U32, name="w2w", align_bytes=64, offset=W2_AT)
-        wgs_sb = late.tile([P, S], F32, name="wgs_sb", offset=WGS_AT)
-        w3w = late.tile([P, GROUPS, 2 * N], U8, name="w3w", align_bytes=64, offset=W3_AT)
+        gain_cols = keep.tile([P, H // P], F32, name="gain_cols")
+        bx_cols = keep.tile([P, H // P], F32, name="bx_cols")
+        warm = placed.tile([P, TAB_AT // 4], F32, name="warm", offset=0)
+        w2w = placed.tile([P, H], U32, name="w2w", align_bytes=64, offset=W2_AT)
+        w2s = placed.tile([P, H], U8, name="w2s", align_bytes=64, offset=W2S_AT)
+        wgs_sb = placed.tile([P, S], F32, name="wgs_sb", offset=WGS_AT)
+        w3w = placed.tile([P, GROUPS, 2 * N], U8, name="w3w", align_bytes=64, offset=W3_AT)
 
-        nc.vector.memset(w2s[:].bitcast(I32), 0)
-        nc.vector.memset(bx_rows[:], 0.0)
         nc.vector.memset(tabs[:].bitcast(I32), 0)
         nc.vector.memset(gain_rows[:], 0.0)
+        nc.vector.memset(bx_rows[:], 0.0)
         nc.vector.memset(w3s[:].rearrange("p a n -> p (a n)").bitcast(I32), 0)
         nc.scalar.activation(out=warm[:, 0:1], in_=gain_rows[:, 0:1], func=ACT.Tanh)
-        load_scale_rows(nc.gpsimd, w2s, w2_scales[0])
+        nc.vector.memset(w2s[:].bitcast(I32), 0)
         make_identity(nc, ident[:])
-        nc.gpsimd.dma_start(out=bx_rows[0:8, :], in_=bx.rearrange("(i p) -> i p", p=P))
+        nc.gpsimd.dma_start(out=bx_rows[0 : H // P, :], in_=bx.rearrange("(i p) -> i p", p=P))
         load_scale_rows(nc.gpsimd, w3s, w3_scales.rearrange("a q n -> q a n"))
 
-        def load_raw(src, width):
-            raw = late.tile([P, 4, width], F32, name="raw", tag="raw", bufs=2, offset=RAW_AT)
+        def load_raw(name, at, src):
+            raw = placed.tile([P, 4, src.shape[1]], F32, name=name, offset=RAW_AT + at)
             nc.sync.dma_start(out=raw[:], in_=src.rearrange("(p t) c -> p t c", t=4))
             return raw
 
         pages = {}
 
-        def load_page(i):
-            pages[i] = late.tile([P, T2], F32, name="page", tag="page", bufs=PAGE_BUFS, offset=0)
-            nc.sync.dma_start(out=pages[i][:], in_=page0[i * P : (i + 1) * P, :])
+        def load_page(tile_no):
+            if tile_no - PAGE_BUFS in (0, 1):
+                at = TAB_AT + (tile_no - PAGE_BUFS) * PAGE_BYTES
+                pages[tile_no] = placed.tile([P, T2], F32, name="page%d" % tile_no, offset=at)
+            else:
+                pages[tile_no] = placed.tile([P, T2], F32, name="page", tag="page", bufs=PAGE_BUFS, offset=0)
+            nc.sync.dma_start(out=pages[tile_no][:], in_=page0[tile_no * P : (tile_no + 1) * P, :])
 
         nc.sync.dma_start(out=list1[:], in_=offs)
         nc.sync.dma_start(out=list2[:], in_=offs2)
         nc.sync.dma_start(out=list3[:], in_=offs3)
         nc.sync.dma_start(out=tabw[:].bitcast(I32), in_=words_of(tab_words[0]))
         load_scale_rows(nc.sync, tabs, tab_scales[0])
-        nc.sync.dma_start(out=gain_rows[0:8, :], in_=gain.rearrange("(i p) -> i p", p=P))
-        w1_raw = [load_raw(w1[:, 0:512], 512)]
-        nc.sync.dma_start(out=w2w[:].bitcast(I32), in_=words_of(w2_words[0]))
-        nc.sync.dma_start(out=wgs_sb[:], in_=wgs)
+        nc.sync.dma_start(out=gain_rows[0 : H // P, :], in_=gain.rearrange("(i p) -> i p", p=P))
+        w1_first = load_raw("w1_first", 0, w1[:, 0:P])
+        nc.sync.dma_start(out=w2w[:, 0:PASS].bitcast(I32), in_=words_of(w2_words[0])[:, 0:PASS])
+        load_scale_rows(nc.sync, w2s, w2_scales[0])
+        w1_rest = load_raw("w1_rest", 4 * P * 4, w1[:, P:PASS])
+        nc.sync.dma_start(out=wgs_sb[:, 0:HALF], in_=wgs[:, 0:HALF])
         load_page(0)
+        w1_second = load_raw("w1_second", RAW_BYTES, w1[:, PASS:H])
         load_page(1)
-        w1_raw.append(load_raw(w1[:, 512:1024], 512))
-        for i in range(2, PAGE_BUFS):
-            load_page(i)
+        nc.sync.dma_start(out=wgs_sb[:, HALF:S], in_=wgs[:, HALF:S])
+        load_page(2)
+        nc.sync.dma_start(out=w2w[:, PASS:H].bitcast(I32), in_=words_of(w2_words[0])[:, PASS:H])
         nc.sync.dma_start(out=w3w[:].bitcast(I32), in_=w3_words.rearrange("a p c -> p a c").bitcast(I32))
-        w4_raw = {a: load_raw(w4[512 * a : 512 * (a + 1), :], N) for a in reversed(range(GROUPS))}
+        load_page(3)
+        load_page(4)
+        w4_raw = [load_raw("w4_%d" % g, g * RAW_BYTES, w4[PASS * g : PASS * (g + 1), :]) for g in range(GROUPS)]
 
-        def interleave(raw, width, piece):
-            grouped = ring.tile([P, 4 * width], BF16, name="grouped", tag="grouped", align_bytes=64)
-            for c in range(0, width, piece):
-                nc.scalar.copy(out=grouped[:, 4 * c : 4 * (c + piece)].rearrange("p (c i t) -> p c t i", i=4, t=4),
-                               in_=raw[:, :, c : c + piece].rearrange("p t (c i) -> p c t i", i=4))
-            return grouped[:]
+        def interleave(copy, grouped, raw, piece):
+            for c in range(0, raw.shape[2], piece):
+                copy(out=grouped[:, 4 * c : 4 * (c + piece)].rearrange("p (c i t) -> p c t i", i=4, t=4),
+                     in_=raw[:, :, c : c + piece].rearrange("p t (c i) -> p c t i", i=4))
+
+        def staging(width):
+            return ring.tile([P, 4 * width], BF16, name="grouped", tag="grouped", align_bytes=64)
 
         def quantize(codes, scales, values):
             nc.vector.quantize_mx(out=codes.bitcast(FP8X4), scales=scales, in_=values)
 
-        w1q = [keep.tile([P, 512], U32, name="w1q%d" % g, align_bytes=64) for g in range(GROUPS)]
-        w1s = [keep.tile([P, 512], U8, name="w1s%d" % g, align_bytes=64) for g in range(GROUPS)]
+        w1q = [keep.tile([P, PASS], U32, name="w1q%d" % g, align_bytes=64) for g in range(GROUPS)]
+        w1s = [keep.tile([P, PASS], U8, name="w1s%d" % g, align_bytes=64) for g in range(GROUPS)]
         w4q = [keep.tile([P, N], U32, name="w4q%d" % g, align_bytes=64) for g in range(GROUPS)]
         w4s = [keep.tile([P, N], U8, name="w4s%d" % g, align_bytes=64) for g in range(GROUPS)]
-        vq = [keep.tile([P, HALF], U32, name="vq%d" % hf, align_bytes=64) for hf in range(2)]
-        vs = [keep.tile([P, HALF], U8, name="vs%d" % hf, align_bytes=64) for hf in range(2)]
-        xq = {(g, hf): keep.tile([P, HALF], U32, name="xq%d%d" % (g, hf), align_bytes=64) for g in range(GROUPS) for hf in range(2)}
-        xs = {(g, hf): keep.tile([P, HALF], U8, name="xs%d%d" % (g, hf), align_bytes=64) for g in range(GROUPS) for hf in range(2)}
+        grouped_first = placed.tile([P, 4 * P], BF16, name="grouped_first", align_bytes=64, offset=V1_AT + 3 * HALF)
+        vq = [keep.tile([P, HALF], U32, name="vq0", align_bytes=64),
+              placed.tile([P, HALF], U32, name="vq1", align_bytes=64, offset=V1_AT)]
+        vs = [keep.tile([P, HALF], U8, name="vs0", align_bytes=64),
+              placed.tile([P, HALF], U8, name="vs1", align_bytes=64, offset=V1_AT + 4 * HALF)]
+        pieces_of_x = [(g, hf) for g in range(GROUPS) for hf in range(2)]
+        xq = {key: keep.tile([P, HALF], U32, name="xq%d%d" % key, align_bytes=64) for key in pieces_of_x}
+        xs = {key: keep.tile([P, HALF], U8, name="xs%d%d" % key, align_bytes=64) for key in pieces_of_x}
 
-        def half_of(lst, hf):
-            return lst[:, hf * (HALF // 16) : (hf + 1) * (HALF // 16)]
+        def half_of(offsets, hf):
+            return offsets[:, hf * (HALF // 16) : (hf + 1) * (HALF // 16)]
 
-        def prepare_w1(g):
-            quantize(w1q[g][:], w1s[g][:], interleave(w1_raw[g], 512, P))
+        def prepare_w1_first():
+            interleave(nc.scalar.copy, grouped_first, w1_first, P)
+            quantize(w1q[0][:, 0:P], w1s[0][:, 0:P], grouped_first[:])
+
+        def prepare_w1_rest():
+            values = staging(PASS - P)
+            interleave(nc.vector.tensor_copy, values, w1_rest, PASS - P)
+            quantize(w1q[0][:, P : 2 * P], w1s[0][:, P : 2 * P], values[:, 0 : 4 * P])
+            quantize(w1q[0][:, 2 * P : PASS], w1s[0][:, 2 * P : PASS], values[:, 4 * P : 4 * (PASS - P)])
+
+        def prepare_w1_second():
+            values = staging(PASS)
+            interleave(nc.scalar.copy, values, w1_second, P)
+            quantize(w1q[1][:], w1s[1][:], values[:])
 
         def prepare_w4(g):
-            values = interleave(w4_raw[g], N, P)
-            quantize(w4q[g][:, 0:512], w4s[g][:, 0:512], values[:, 0:2048])
-            quantize(w4q[g][:, 512:N], w4s[g][:, 512:N], values[:, 2048 : 4 * N])
+            values = staging(N)
+            interleave(nc.scalar.copy, values, w4_raw[g], P)
+            quantize(w4q[g][:, 0:BANK], w4s[g][:, 0:BANK], values[:, 0 : 4 * BANK])
+            quantize(w4q[g][:, BANK:N], w4s[g][:, BANK:N], values[:, 4 * BANK : 4 * N])
 
         def gather_table(hf):
             nc.vector.tensor_copy(out=vq[hf][:], in_=tabw[:].indirect(half_of(list1, hf)))
             nc.vector.tensor_copy(out=vs[hf][:], in_=tabs[:].indirect(half_of(list1, hf)))
 
-        def bank(tag):
+        def bank():
             return psum.tile([P, BANK], F32, name="bank", tag="bank")
 
-        def add_transposed(out, first, second):
-            nc.tensor.matmul(out, lhsT=first, rhs=ident[:], is_transpose=True, start=True, stop=False)
-            nc.tensor.matmul(out, lhsT=second, rhs=ident[:], is_transpose=True, start=False, stop=True)
+        def transpose_into(out, source, start, stop):
+            nc.tensor.matmul(out, lhsT=source, rhs=ident[:], is_transpose=True, start=start, stop=stop)
 
-        sq, bt, h = {}, {}, {}
+        def to_columns(cols, rows):
+            cols_ps = bank()
+            nc.tensor.transpose(cols_ps[:, 0:P], rows[:], ident[:])
+            nc.scalar.copy(out=cols[:], in_=cols_ps[:, 0 : H // P])
 
-        def products(g, hf, jb, copy):
-            cj = slice(jb * P, (jb + 1) * P)
-            cr = slice(g * 512, (g + 1) * 512)
-            a_ps, b_ps = bank("mm"), bank("mm")
-            nc.tensor.matmul_mx(out=a_ps[:], lhsT=vq[hf][:, cj].bitcast(FP8X4), lhsT_scale=vs[hf][:, cj],
-                                rhs=w1q[g][:].bitcast(FP8X4), rhs_scale=w1s[g][:], start=True, stop=True)
-            nc.tensor.matmul_mx(out=b_ps[:], lhsT=vq[hf][:, cj].bitcast(FP8X4), lhsT_scale=vs[hf][:, cj],
-                                rhs=w2w[:, cr].bitcast(FP8X4), rhs_scale=w2s[:, cr], start=True, stop=True)
-            sq[jb] = ring.tile([P, BANK], F32, name="sq", tag="sq", bufs=4)
-            bt[jb] = ring.tile([P, BANK], F32, name="bt", tag="bt", bufs=4)
-            nc.scalar.activation(out=sq[jb][:], in_=a_ps[:], func=ACT.Square)
-            copy(out=bt[jb][:], in_=b_ps[:])
+        parts, h = {}, {}
+
+        def product(name, hf, blocks, tiles, codes, scales):
+            width = len(tiles) * P
+            rows = slice(tiles.start * P, tiles.stop * P)
+            turned_ps = bank()
+            held = ring.tile([P, BANK], F32, name=name, tag=name, bufs=BLOCKS)
+            for n, jb in enumerate(blocks):
+                entries = slice(jb * P, (jb + 1) * P)
+                nc.tensor.matmul_mx(out=turned_ps[:, n * width : (n + 1) * width], lhsT=vq[hf][:, entries].bitcast(FP8X4),
+                                    lhsT_scale=vs[hf][:, entries], rhs=codes[:, rows].bitcast(FP8X4),
+                                    rhs_scale=scales[:, rows], start=True, stop=True)
+                for m, i in enumerate(tiles):
+                    parts[name, jb, i] = held[:, n * width + m * P : n * width + (m + 1) * P]
+            return held, turned_ps
+
+        def square_a(g, hf, blocks, tiles):
+            held, turned_ps = product("sq", hf, blocks, tiles, w1q[g], w1s[g])
+            nc.scalar.activation(out=held[:], in_=turned_ps[:], func=ACT.Square)
+
+        def copy_b(g, hf, blocks, tiles):
+            rows = slice(g * PASS, (g + 1) * PASS)
+            held, turned_ps = product("bt", hf, blocks, tiles, w2w[:, rows], w2s[:, rows])
+            nc.scalar.copy(out=held[:], in_=turned_ps[:])
+
+        def products(g, hf):
+            for jb in range(BLOCKS):
+                square_a(g, hf, range(jb, jb + 1), range(TILES))
+                copy_b(g, hf, range(jb, jb + 1), range(TILES))
 
         def make_h(g, hf, i):
-            h_ps = bank("tr")
-            cr = slice(i * P, (i + 1) * P)
-            for jb in range(4):
-                add_transposed(h_ps[:, jb * P : (jb + 1) * P], sq[jb][:, cr], bt[jb][:, cr])
-            h[g, hf, i] = ring.tile([P, HALF], F32, name="h", tag="h", bufs=8)
             tile_no = TILES * g + i
+            h_ps = bank()
+            for jb in range(BLOCKS):
+                transpose_into(h_ps[:, jb * P : (jb + 1) * P], parts["sq", jb, i], True, False)
+                transpose_into(h_ps[:, jb * P : (jb + 1) * P], parts["bt", jb, i], False, True)
+            h[g, hf, i] = ring.tile([P, HALF], F32, name="h", tag="h", bufs=2 * TILES)
             nc.scalar.activation(out=h[g, hf, i][:], in_=h_ps[:], func=ACT.Copy, scale=gain_cols[:, tile_no : tile_no + 1])
-
-        def produce(g, hf, copy):
-            for jb in range(4):
-                products(g, hf, jb, copy)
-            for i in range(TILES):
-                make_h(g, hf, i)
 
         def scatter(g, hf, i):
             nc.vector.tensor_tensor(out=pages[TILES * g + i][:].indirect(half_of(list2, hf)), in0=h[g, hf, i][:],
                                     in1=wgs_sb[:, hf * HALF : (hf + 1) * HALF], op=ALU.mult)
 
-        def round_sorted(copy, turned, i, turned_ps):
-            copy(
+        def store_page(tile_no):
+            nc.sync.dma_start(out=out_1[tile_no * P : (tile_no + 1) * P, :], in_=pages[tile_no][:])
+
+        def round_sorted(turned, i, turned_ps):
+            nc.scalar.copy(
                 out=turned[:].rearrange("m b (u p e) -> m b u p e", u=2, e=2)[:, :, :, 32 * i : 32 * (i + 1), :],
-                in_=turned_ps[:].rearrange("m (b p u e) -> m b u p e", b=4, u=2, e=2),
+                in_=turned_ps[:].rearrange("m (b p u e) -> m b u p e", b=BLOCKS, u=2, e=2),
             )
 
-        def turn_back(turned, copies):
+        def turn_back(turned):
             words = turned[:].rearrange("m b r -> m (b r)").bitcast(F32)
-            woven = ring.tile([P, 4 * BANK], BF16, name="woven", tag="woven", bufs=6, align_bytes=64)
+            woven = ring.tile([P, 4 * BANK], BF16, name="woven", tag="woven", bufs=2 + QUARTERS, align_bytes=64)
             woven_words = woven[:].bitcast(F32)
             for pair in range(2):
-                back_ps = bank("tr")
-                for s in range(4):
-                    src = (4 * pair + s) * P
-                    nc.tensor.transpose(back_ps[:, s * P : (s + 1) * P], words[:, src : src + P], ident[:])
-                copies[pair](
+                back_ps = bank()
+                for n in range(BLOCKS):
+                    src = (BLOCKS * pair + n) * P
+                    nc.tensor.transpose(back_ps[:, n * P : (n + 1) * P], words[:, src : src + P], ident[:])
+                nc.scalar.copy(
                     out=woven_words[:, pair * BANK : (pair + 1) * BANK].rearrange("p (b m u) -> p b m u", b=2, u=2),
                     in_=back_ps[:].rearrange("p (b u m) -> p b m u", b=2, u=2),
                 )
             return woven
 
-        x_turned, page_turned, picked = {}, {}, {}
+        picked, x_banks, x_turned, page_turned = {}, {}, {}, {}
 
-        def pick(g, hf, i):
-            picked[i, hf] = ring.tile([P, HALF], F32, name="picked", tag="picked", bufs=8)
-            nc.vector.tensor_copy(out=picked[i, hf][:], in_=pages[TILES * g + i][:].indirect(half_of(list3, hf)))
+        def pick(g, i, pieces):
+            picked[i] = ring.tile([P, PX], F32, name="picked", tag="picked", bufs=TILES)
+            width = PX // pieces
+            for at in range(0, PX, width):
+                nc.vector.tensor_copy(out=picked[i][:, at : at + width],
+                                      in_=pages[TILES * g + i][:].indirect(list3[:, at // 16 : (at + width) // 16]))
 
-        def turn_x(g, hf, i, copy):
+        def spread_bias(g, hf, i):
+            x_banks[hf] = bank()
+            tile_no = TILES * g + i
+            for jb in range(BLOCKS):
+                transpose_into(x_banks[hf][:, jb * P : (jb + 1) * P],
+                               bx_cols[:, tile_no : tile_no + 1].to_broadcast([P, P]), jb == 0, False)
+
+        def add_picked(hf, i):
             if i == 0:
-                x_turned[hf] = ring.tile([P, 4, 512], BF16, name="x_turned", tag="x_turned")
-            x_ps = bank("tr")
-            col = TILES * g + i
-            for jb in range(4):
-                nc.tensor.matmul(x_ps[:, jb * P : (jb + 1) * P], lhsT=bx_cols[:, col : col + 1].to_broadcast([P, P]),
-                                 rhs=ident[:], is_transpose=True, start=(jb == 0), stop=False)
-            for jb in range(4):
-                nc.tensor.matmul(x_ps[:, jb * P : (jb + 1) * P], lhsT=picked[i, hf][:, jb * P : (jb + 1) * P],
-                                 rhs=ident[:], is_transpose=True, start=False, stop=(jb == 3))
-            round_sorted(copy, x_turned[hf], i, x_ps)
+                x_turned[hf] = ring.tile([P, BLOCKS, PASS], BF16, name="x_turned", tag="x_turned")
+            for jb in range(BLOCKS):
+                src = hf * HALF + jb * P
+                transpose_into(x_banks[hf][:, jb * P : (jb + 1) * P], picked[i][:, src : src + P], False, jb == BLOCKS - 1)
+            round_sorted(x_turned[hf], i, x_banks[hf])
+
+        def turn_x(g, i):
+            for hf in range(2):
+                spread_bias(g, hf, i)
+                add_picked(hf, i)
 
         def turn_page(g, i, quarter):
             if i == 0:
-                page_turned[quarter] = ring.tile([P, 4, 512], BF16, name="page_turned", tag="page_turned", bufs=4)
-            page_ps = bank("tr")
-            for b in range(4):
-                src = (4 * quarter + b) * P
+                page_turned[quarter] = ring.tile([P, BLOCKS, PASS], BF16, name="page_turned", tag="page_turned", bufs=QUARTERS)
+            page_ps = bank()
+            for b in range(BLOCKS):
+                src = (BLOCKS * quarter + b) * P
                 nc.tensor.transpose(page_ps[:, b * P : (b + 1) * P], pages[TILES * g + i][:, src : src + P], ident[:])
-            round_sorted(nc.scalar.copy, page_turned[quarter], i, page_ps)
+            round_sorted(page_turned[quarter], i, page_ps)
 
-        def store_page(tile_no):
-            nc.sync.dma_start(out=out_1[tile_no * P : (tile_no + 1) * P, :], in_=pages[tile_no][:])
+        def finish_x(g, hf):
+            quantize(xq[g, hf][:], xs[g, hf][:], turn_back(x_turned[hf])[:])
 
-        def finish_x(g, hf, copies):
-            quantize(xq[g, hf][:], xs[g, hf][:], turn_back(x_turned[hf], copies)[:])
-
-        plane_words, plane_scales = {}, {}
+        page_q, page_s = {}, {}
 
         def finish_page(g, quarter):
             if quarter == 0:
-                plane_words[g] = ring.tile([P, T2], U32, name="plane_words", tag="plane_words", bufs=1, align_bytes=64)
-                plane_scales[g] = ring.tile([P, T2], U8, name="plane_scales", tag="plane_scales", bufs=1, align_bytes=64)
-            cm = slice(quarter * 512, (quarter + 1) * 512)
-            quantize(plane_words[g][:, cm], plane_scales[g][:, cm], turn_back(page_turned[quarter], on_scalar)[:])
-            nc.sync.dma_start(out=words_of(out_2[g])[:, cm], in_=plane_words[g][:, cm].bitcast(I32))
-            if quarter == 3:
+                page_q[g] = ring.tile([P, T2], U32, name="page_q", tag="page_q", bufs=1, align_bytes=64)
+                page_s[g] = ring.tile([P, T2], U8, name="page_s", tag="page_s", bufs=1, align_bytes=64)
+            columns = slice(quarter * BANK, (quarter + 1) * BANK)
+            quantize(page_q[g][:, columns], page_s[g][:, columns], turn_back(page_turned[quarter])[:])
+            nc.sync.dma_start(out=words_of(out_2[g])[:, columns], in_=page_q[g][:, columns].bitcast(I32))
+            if quarter == QUARTERS - 1:
                 for q in range(4):
                     nc.sync.dma_start(out=out_3[g, 4 * q : 4 * q + 4, :].bitcast(I32),
-                                      in_=plane_scales[g][32 * q : 32 * q + 4, :].bitcast(I32))
+                                      in_=page_s[g][32 * q : 32 * q + 4, :].bitcast(I32))
 
-        second = {}
+        sums, gated = {}, {}
 
-        def second_products(hf, nt):
-            c_ps, e_ps = bank("mm"), bank("tr")
-            cn = slice(nt * P, (nt + 1) * P)
-            for g in reversed(range(GROUPS)):
-                nc.tensor.matmul_mx(out=c_ps[:], lhsT=w3w[:, g, 2 * nt * P : 2 * (nt + 1) * P].bitcast(FP4X4),
-                                    lhsT_scale=w3s[:, g, cn], rhs=xq[g, hf][:].bitcast(FP8X4), rhs_scale=xs[g, hf][:],
-                                    start=(g == GROUPS - 1), stop=(g == 0))
-            for g in reversed(range(GROUPS)):
-                nc.tensor.matmul_mx(out=e_ps[:], lhsT=w4q[g][:, cn].bitcast(FP8X4), lhsT_scale=w4s[g][:, cn],
-                                    rhs=xq[g, hf][:].bitcast(FP8X4), rhs_scale=xs[g, hf][:],
-                                    start=(g == GROUPS - 1), stop=(g == 0))
-            th = ring.tile([P, BANK], F32, name="th", tag="sq", bufs=4)
-            nc.scalar.activation(out=th[:], in_=c_ps[:], func=ACT.Tanh)
-            gated = ring.tile([P, BANK], F32, name="gated", tag="bt", bufs=4)
-            nc.vector.tensor_tensor(out=gated[:], in0=e_ps[:], in1=th[:], op=ALU.mult)
-            second[hf, nt] = (c_ps, gated)
+        def second_pass(hf, nt, g):
+            if g == 0:
+                sums[hf, nt] = (bank(), bank())
+            y1_ps, y2_ps = sums[hf, nt]
+            outs = slice(nt * P, (nt + 1) * P)
+            nc.tensor.matmul_mx(out=y1_ps[:], lhsT=w3w[:, g, 2 * nt * P : 2 * (nt + 1) * P].bitcast(FP4X4),
+                                lhsT_scale=w3s[:, g, outs], rhs=xq[g, hf][:].bitcast(FP8X4), rhs_scale=xs[g, hf][:],
+                                start=(g == 0), stop=(g == GROUPS - 1))
+            nc.tensor.matmul_mx(out=y2_ps[:], lhsT=w4q[g][:, outs].bitcast(FP8X4), lhsT_scale=w4s[g][:, outs],
+                                rhs=xq[g, hf][:].bitcast(FP8X4), rhs_scale=xs[g, hf][:],
+                                start=(g == 0), stop=(g == GROUPS - 1))
 
-        def second_sum(hf, nt):
-            c_ps, gated = second[hf, nt]
-            y = ring.tile([P, BANK], F32, name="y", tag="h", bufs=8)
-            nc.vector.tensor_tensor(out=y[:], in0=c_ps[:], in1=gated[:], op=ALU.add)
+        def gate(hf, nt):
+            y1_ps, y2_ps = sums[hf, nt]
+            th = ring.tile([P, BANK], F32, name="th", tag="sq", bufs=BLOCKS)
+            nc.scalar.activation(out=th[:], in_=y1_ps[:], func=ACT.Tanh)
+            gated[hf, nt] = ring.tile([P, BANK], F32, name="gated", tag="bt", bufs=BLOCKS)
+            nc.vector.tensor_tensor(out=gated[hf, nt][:], in0=y2_ps[:], in1=th[:], op=ALU.mult)
+
+        def finish_y(hf, nt):
+            y = ring.tile([P, BANK], F32, name="y", tag="h", bufs=2 * TILES)
+            nc.vector.tensor_tensor(out=y[:], in0=sums[hf, nt][0][:], in1=gated[hf, nt][:], op=ALU.add)
             nc.sync.dma_start(out=out_0[nt * P : (nt + 1) * P, hf * HALF : (hf + 1) * HALF], in_=y[:])
 
-        on_scalar = (nc.scalar.copy, nc.scalar.copy)
-
-        def to_columns(cols, rows):
-            cols_ps = bank("tr")
-            nc.tensor.transpose(cols_ps[:, 0:P], rows[:], ident[:])
-            nc.scalar.copy(out=cols[:], in_=cols_ps[:, 0:8])
-
-        def picks(g, i):
-            for hf in range(2):
-                pick(g, hf, i)
-
-        def turns(g, i):
-            for hf in range(2):
-                turn_x(g, hf, i, nc.scalar.copy)
-
-        def page_turns(g, i):
-            for quarter in range(4):
-                turn_page(g, i, quarter)
+        last = TILES - 1
+        every_block = range(BLOCKS)
 
         gather_table(0)
-        gather_table(1)
-        prepare_w1(0)
+        prepare_w1_first()
         to_columns(gain_cols, gain_rows)
-        produce(0, 0, nc.vector.tensor_copy)
-        prepare_w1(1)
-        produce(0, 1, nc.scalar.copy)
+        gather_table(1)
+        square_a(0, 0, every_block, range(0, 1))
+        copy_b(0, 0, every_block, range(0, 1))
+        copy_b(0, 0, every_block, range(1, 2))
+        make_h(0, 0, 0)
+        prepare_w1_rest()
+        for i in range(2, TILES):
+            copy_b(0, 0, every_block, range(i, i + 1))
+        for i in range(1, TILES):
+            square_a(0, 0, every_block, range(i, i + 1))
+        for i in range(1, TILES):
+            make_h(0, 0, i)
+        prepare_w1_second()
+        products(0, 1)
+        for i in range(TILES):
+            make_h(0, 1, i)
         to_columns(bx_cols, bx_rows)
         for i in range(TILES):
             scatter(0, 0, i)
-        produce(1, 0, nc.scalar.copy)
-        for jb in range(4):
-            products(1, 1, jb, nc.scalar.copy)
-        last = TILES - 1
+        load_page(PAGE_BUFS)
+        load_page(PAGE_BUFS + 1)
+        products(1, 0)
+        for i in range(TILES):
+            make_h(1, 0, i)
+        products(1, 1)
 
-        def second_half(g):
+        def complete_tiles(g):
+            final = g == GROUPS - 1
             for i in range(TILES):
                 if i == last:
-                    picks(g, i - 1)
-                    turns(g, i - 1)
+                    pick(g, i - 1, 1)
+                    turn_x(g, i - 1)
                 scatter(g, 1, i)
                 store_page(TILES * g + i)
+                if not (final and i == last):
+                    for quarter in range(QUARTERS):
+                        turn_page(g, i, quarter)
                 if 0 < i < last:
-                    picks(g, i - 1)
-                    turns(g, i - 1)
-                if g == 0 or i < last:
-                    page_turns(g, i)
-                if g == 0 and i > 0:
-                    load_page(TILES + i)
-            picks(g, last)
+                    pick(g, i - 1, 1)
+                    turn_x(g, i - 1)
+                if g == 0 and i == 1:
+                    load_page(GROUPS * TILES - 1)
+            pick(g, last, 2 if final else 1)
 
-        second_half(0)
-        turns(0, last)
-        for i in range(TILES):
-            scatter(1, 0, i)
-        for hf in range(2):
-            finish_x(0, hf, on_scalar)
-        for quarter in range(4):
-            finish_page(0, quarter)
+        complete_tiles(0)
+        turn_x(0, last)
         for i in range(TILES):
             make_h(1, 1, i)
-        for g in reversed(range(GROUPS)):
+        for i in range(TILES):
+            scatter(1, 0, i)
+        for g in range(GROUPS):
             prepare_w4(g)
-        second_half(1)
-        for quarter in range(2):
-            turn_page(1, last, quarter)
-        turn_x(1, 0, last, nc.scalar.copy)
-        turn_page(1, last, 2)
-        turn_x(1, 1, last, nc.vector.tensor_copy)
-        finish_x(1, 0, (nc.scalar.copy, nc.vector.tensor_copy))
-        turn_page(1, last, 3)
-        finish_x(1, 1, (nc.scalar.copy, nc.vector.tensor_copy))
-        finish_page(1, 0)
+        for hf in range(2):
+            finish_x(0, hf)
+        for quarter in range(QUARTERS):
+            finish_page(0, quarter)
+        complete_tiles(1)
+
+        for hf in range(2):
+            spread_bias(1, hf, last)
+        turn_page(1, last, 0)
+        for hf in range(2):
+            turn_page(1, last, 1 + hf)
+            add_picked(hf, last)
+        finish_x(1, 0)
         steps = [(hf, nt) for hf in range(2) for nt in range(N // P)]
-        for s, (hf, nt) in enumerate(steps):
-            second_products(hf, nt)
-            if s > 0:
-                second_sum(*steps[s - 1])
-            if s in (1, 3, 5):
-                finish_page(1, (s + 1) // 2)
-        second_sum(*steps[-1])
+        early = steps[:2]
+        for hf, nt in early:
+            second_pass(hf, nt, 0)
+        turn_page(1, last, QUARTERS - 1)
+
+        for n, (hf, nt) in enumerate(steps):
+            if (hf, nt) not in early:
+                second_pass(hf, nt, 0)
+            second_pass(hf, nt, 1)
+            gate(hf, nt)
+            if n > 0:
+                finish_y(*steps[n - 1])
+            if n == len(early) - 1:
+                finish_x(1, 1)
+            if n >= len(early) and n % 2 == 0:
+                finish_page(1, (n - len(early)) // 2)
+        finish_y(*steps[-1])

from contextlib import ExitStack

import concourse.mybir as mybir
from concourse.masks import make_identity

K, H, N, T, S, T2, PX = 512, 1024, 640, 4096, 1024, 2048, 1024
FLOPS = 2 * (2 * K * H * S + 2 * H * N * PX)

F32 = mybir.dt.float32
BF16 = mybir.dt.bfloat16
I32 = mybir.dt.int32
U32 = mybir.dt.uint32
U16 = mybir.dt.uint16
U8 = mybir.dt.uint8
FP8X4 = mybir.dt.float8_e4m3fn_x4
FP4X4 = mybir.dt.float4_e2m1fn_x4
ACT = mybir.ActivationFunctionType
ALU = mybir.AluOpType

P = 128
PASS = 512
BANK = 512
HALF = 512
BLOCKS = BANK // P
GROUPS = H // PASS
TILES = PASS // P
QUARTERS = T2 // BANK

PAGE_BYTES = T2 * 4
PAGE_BUFS = 5
RAW_AT = PAGE_BUFS * PAGE_BYTES
RAW_BYTES = 4 * N * 4
W2_AT = RAW_AT + 2 * RAW_BYTES
W2S_AT = W2_AT + H * 4
WGS_AT = W2S_AT + H
W3_AT = WGS_AT + S * 4
TAB_AT = W3_AT + GROUPS * 2 * N
V1_AT = TAB_AT + T * 4


def tile_list_aligner_stage_cells_kernel(
    tc, tab_words, tab_scales, offs, offs2, offs3, w1, w2_words, w2_scales, gain, page0, wgs, bx,
    w3_words, w3_scales, w4, out_0, out_1, out_2, out_3,
):
    nc = tc.nc
    with ExitStack() as ctx:
        keep = ctx.enter_context(tc.tile_pool(name="keep", bufs=1))
        ring = ctx.enter_context(tc.tile_pool(name="ring", bufs=2))
        placed = ctx.enter_context(tc.tile_pool(name="placed", bufs=1))
        psum = ctx.enter_context(tc.psum_pool(name="psum", bufs=8))

        def words_of(dram_words):
            return dram_words.rearrange("p c i -> p (c i)").bitcast(I32)

        def load_scale_rows(queue, plane, rows):
            for q in range(4):
                queue.dma_start(out=plane[32 * q : 32 * q + 4].bitcast(I32), in_=rows[4 * q : 4 * q + 4].bitcast(I32))

        list1 = keep.tile([P, S // 16], U16, name="list1")
        list2 = keep.tile([P, S // 16], U16, name="list2")
        list3 = keep.tile([P, PX // 16], U16, name="list3")
        tabw = placed.tile([P, T], U32, name="tabw", align_bytes=64, offset=TAB_AT)
        tabs = keep.tile([P, T], U8, name="tabs", align_bytes=64)
        w3s = keep.tile([P, GROUPS, N], U8, name="w3s", align_bytes=64)
        ident = keep.tile([P, P], F32, name="ident")
        gain_rows = keep.tile([P, P], F32, name="gain_rows")
        bx_rows = keep.tile([P, P], F32, name="bx_rows")
        gain_cols = keep.tile([P, H // P], F32, name="gain_cols")
        bx_cols = keep.tile([P, H // P], F32, name="bx_cols")
        warm = placed.tile([P, TAB_AT // 4], F32, name="warm", offset=0)
        w2w = placed.tile([P, H], U32, name="w2w", align_bytes=64, offset=W2_AT)
        w2s = placed.tile([P, H], U8, name="w2s", align_bytes=64, offset=W2S_AT)
        wgs_sb = placed.tile([P, S], F32, name="wgs_sb", offset=WGS_AT)
        w3w = placed.tile([P, GROUPS, 2 * N], U8, name="w3w", align_bytes=64, offset=W3_AT)

        nc.vector.memset(tabs[:].bitcast(I32), 0)
        nc.vector.memset(gain_rows[:], 0.0)
        nc.vector.memset(bx_rows[:], 0.0)
        nc.vector.memset(w3s[:].rearrange("p a n -> p (a n)").bitcast(I32), 0)
        nc.scalar.activation(out=warm[:, 0:1], in_=gain_rows[:, 0:1], func=ACT.Tanh)
        nc.vector.memset(w2s[:].bitcast(I32), 0)
        make_identity(nc, ident[:])
        nc.gpsimd.dma_start(out=bx_rows[0 : H // P, :], in_=bx.rearrange("(i p) -> i p", p=P))
        load_scale_rows(nc.gpsimd, w3s, w3_scales.rearrange("a q n -> q a n"))

        def load_raw(name, at, src):
            raw = placed.tile([P, 4, src.shape[1]], F32, name=name, offset=RAW_AT + at)
            nc.sync.dma_start(out=raw[:], in_=src.rearrange("(p t) c -> p t c", t=4))
            return raw

        pages = {}

        def load_page(tile_no):
            if tile_no - PAGE_BUFS in (0, 1):
                at = TAB_AT + (tile_no - PAGE_BUFS) * PAGE_BYTES
                pages[tile_no] = placed.tile([P, T2], F32, name="page%d" % tile_no, offset=at)
            else:
                pages[tile_no] = placed.tile([P, T2], F32, name="page", tag="page", bufs=PAGE_BUFS, offset=0)
            nc.sync.dma_start(out=pages[tile_no][:], in_=page0[tile_no * P : (tile_no + 1) * P, :])

        nc.sync.dma_start(out=list1[:], in_=offs)
        nc.sync.dma_start(out=list2[:], in_=offs2)
        nc.sync.dma_start(out=list3[:], in_=offs3)
        nc.sync.dma_start(out=tabw[:].bitcast(I32), in_=words_of(tab_words[0]))
        load_scale_rows(nc.sync, tabs, tab_scales[0])
        nc.sync.dma_start(out=gain_rows[0 : H // P, :], in_=gain.rearrange("(i p) -> i p", p=P))
        w1_first = load_raw("w1_first", 0, w1[:, 0:P])
        nc.sync.dma_start(out=w2w[:, 0:PASS].bitcast(I32), in_=words_of(w2_words[0])[:, 0:PASS])
        load_scale_rows(nc.sync, w2s, w2_scales[0])
        w1_rest = load_raw("w1_rest", 4 * P * 4, w1[:, P:PASS])
        nc.sync.dma_start(out=wgs_sb[:, 0:HALF], in_=wgs[:, 0:HALF])
        load_page(0)
        w1_second = load_raw("w1_second", RAW_BYTES, w1[:, PASS:H])
        load_page(1)
        nc.sync.dma_start(out=wgs_sb[:, HALF:S], in_=wgs[:, HALF:S])
        load_page(2)
        nc.sync.dma_start(out=w2w[:, PASS:H].bitcast(I32), in_=words_of(w2_words[0])[:, PASS:H])
        nc.sync.dma_start(out=w3w[:].bitcast(I32), in_=w3_words.rearrange("a p c -> p a c").bitcast(I32))
        load_page(3)
        load_page(4)
        w4_raw = [load_raw("w4_%d" % g, g * RAW_BYTES, w4[PASS * g : PASS * (g + 1), :]) for g in range(GROUPS)]

        def interleave(copy, grouped, raw, piece):
            for c in range(0, raw.shape[2], piece):
                copy(out=grouped[:, 4 * c : 4 * (c + piece)].rearrange("p (c i t) -> p c t i", i=4, t=4),
                     in_=raw[:, :, c : c + piece].rearrange("p t (c i) -> p c t i", i=4))

        def staging(width):
            return ring.tile([P, 4 * width], BF16, name="grouped", tag="grouped", align_bytes=64)

        def quantize(codes, scales, values):
            nc.vector.quantize_mx(out=codes.bitcast(FP8X4), scales=scales, in_=values)

        w1q = [keep.tile([P, PASS], U32, name="w1q%d" % g, align_bytes=64) for g in range(GROUPS)]
        w1s = [keep.tile([P, PASS], U8, name="w1s%d" % g, align_bytes=64) for g in range(GROUPS)]
        w4q = [keep.tile([P, N], U32, name="w4q%d" % g, align_bytes=64) for g in range(GROUPS)]
        w4s = [keep.tile([P, N], U8, name="w4s%d" % g, align_bytes=64) for g in range(GROUPS)]
        grouped_first = placed.tile([P, 4 * P], BF16, name="grouped_first", align_bytes=64, offset=V1_AT + 3 * HALF)
        vq = [keep.tile([P, HALF], U32, name="vq0", align_bytes=64),
              placed.tile([P, HALF], U32, name="vq1", align_bytes=64, offset=V1_AT)]
        vs = [keep.tile([P, HALF], U8, name="vs0", align_bytes=64),
              placed.tile([P, HALF], U8, name="vs1", align_bytes=64, offset=V1_AT + 4 * HALF)]
        pieces_of_x = [(g, hf) for g in range(GROUPS) for hf in range(2)]
        xq = {key: keep.tile([P, HALF], U32, name="xq%d%d" % key, align_bytes=64) for key in pieces_of_x}
        xs = {key: keep.tile([P, HALF], U8, name="xs%d%d" % key, align_bytes=64) for key in pieces_of_x}

        def half_of(offsets, hf):
            return offsets[:, hf * (HALF // 16) : (hf + 1) * (HALF // 16)]

        def prepare_w1_first():
            interleave(nc.scalar.copy, grouped_first, w1_first, P)
            quantize(w1q[0][:, 0:P], w1s[0][:, 0:P], grouped_first[:])

        def prepare_w1_rest():
            values = staging(PASS - P)
            interleave(nc.vector.tensor_copy, values, w1_rest, PASS - P)
            quantize(w1q[0][:, P : 2 * P], w1s[0][:, P : 2 * P], values[:, 0 : 4 * P])
            quantize(w1q[0][:, 2 * P : PASS], w1s[0][:, 2 * P : PASS], values[:, 4 * P : 4 * (PASS - P)])

        def prepare_w1_second():
            values = staging(PASS)
            interleave(nc.scalar.copy, values, w1_second, P)
            quantize(w1q[1][:], w1s[1][:], values[:])

        def prepare_w4(g):
            values = staging(N)
            interleave(nc.scalar.copy, values, w4_raw[g], P)
            quantize(w4q[g][:, 0:BANK], w4s[g][:, 0:BANK], values[:, 0 : 4 * BANK])
            quantize(w4q[g][:, BANK:N], w4s[g][:, BANK:N], values[:, 4 * BANK : 4 * N])

        def gather_table(hf):
            nc.vector.tensor_copy(out=vq[hf][:], in_=tabw[:].indirect(half_of(list1, hf)))
            nc.vector.tensor_copy(out=vs[hf][:], in_=tabs[:].indirect(half_of(list1, hf)))

        def bank():
            return psum.tile([P, BANK], F32, name="bank", tag="bank")

        def transpose_into(out, source, start, stop):
            nc.tensor.matmul(out, lhsT=source, rhs=ident[:], is_transpose=True, start=start, stop=stop)

        def to_columns(cols, rows):
            cols_ps = bank()
            nc.tensor.transpose(cols_ps[:, 0:P], rows[:], ident[:])
            nc.scalar.copy(out=cols[:], in_=cols_ps[:, 0 : H // P])

        parts, h = {}, {}

        def product(name, hf, blocks, tiles, codes, scales):
            width = len(tiles) * P
            rows = slice(tiles.start * P, tiles.stop * P)
            turned_ps = bank()
            held = ring.tile([P, BANK], F32, name=name, tag=name, bufs=BLOCKS)
            for n, jb in enumerate(blocks):
                entries = slice(jb * P, (jb + 1) * P)
                nc.tensor.matmul_mx(out=turned_ps[:, n * width : (n + 1) * width], lhsT=vq[hf][:, entries].bitcast(FP8X4),
                                    lhsT_scale=vs[hf][:, entries], rhs=codes[:, rows].bitcast(FP8X4),
                                    rhs_scale=scales[:, rows], start=True, stop=True)
                for m, i in enumerate(tiles):
                    parts[name, jb, i] = held[:, n * width + m * P : n * width + (m + 1) * P]
            return held, turned_ps

        def square_a(g, hf, blocks, tiles):
            held, turned_ps = product("sq", hf, blocks, tiles, w1q[g], w1s[g])
            nc.scalar.activation(out=held[:], in_=turned_ps[:], func=ACT.Square)

        def copy_b(g, hf, blocks, tiles):
            rows = slice(g * PASS, (g + 1) * PASS)
            held, turned_ps = product("bt", hf, blocks, tiles, w2w[:, rows], w2s[:, rows])
            nc.scalar.copy(out=held[:], in_=turned_ps[:])

        def products(g, hf):
            for jb in range(BLOCKS):
                square_a(g, hf, range(jb, jb + 1), range(TILES))
                copy_b(g, hf, range(jb, jb + 1), range(TILES))

        def make_h(g, hf, i):
            tile_no = TILES * g + i
            h_ps = bank()
            for jb in range(BLOCKS):
                transpose_into(h_ps[:, jb * P : (jb + 1) * P], parts["sq", jb, i], True, False)
                transpose_into(h_ps[:, jb * P : (jb + 1) * P], parts["bt", jb, i], False, True)
            h[g, hf, i] = ring.tile([P, HALF], F32, name="h", tag="h", bufs=2 * TILES)
            nc.scalar.activation(out=h[g, hf, i][:], in_=h_ps[:], func=ACT.Copy, scale=gain_cols[:, tile_no : tile_no + 1])

        def scatter(g, hf, i):
            nc.vector.tensor_tensor(out=pages[TILES * g + i][:].indirect(half_of(list2, hf)), in0=h[g, hf, i][:],
                                    in1=wgs_sb[:, hf * HALF : (hf + 1) * HALF], op=ALU.mult)

        def store_page(tile_no):
            nc.sync.dma_start(out=out_1[tile_no * P : (tile_no + 1) * P, :], in_=pages[tile_no][:])

        def round_sorted(turned, i, turned_ps):
            nc.scalar.copy(
                out=turned[:].rearrange("m b (u p e) -> m b u p e", u=2, e=2)[:, :, :, 32 * i : 32 * (i + 1), :],
                in_=turned_ps[:].rearrange("m (b p u e) -> m b u p e", b=BLOCKS, u=2, e=2),
            )

        def turn_back(turned):
            words = turned[:].rearrange("m b r -> m (b r)").bitcast(F32)
            woven = ring.tile([P, 4 * BANK], BF16, name="woven", tag="woven", bufs=2 + QUARTERS, align_bytes=64)
            woven_words = woven[:].bitcast(F32)
            for pair in range(2):
                back_ps = bank()
                for n in range(BLOCKS):
                    src = (BLOCKS * pair + n) * P
                    nc.tensor.transpose(back_ps[:, n * P : (n + 1) * P], words[:, src : src + P], ident[:])
                nc.scalar.copy(
                    out=woven_words[:, pair * BANK : (pair + 1) * BANK].rearrange("p (b m u) -> p b m u", b=2, u=2),
                    in_=back_ps[:].rearrange("p (b u m) -> p b m u", b=2, u=2),
                )
            return woven

        picked, x_banks, x_turned, page_turned = {}, {}, {}, {}

        def pick(g, i, pieces):
            picked[i] = ring.tile([P, PX], F32, name="picked", tag="picked", bufs=TILES)
            width = PX // pieces
            for at in range(0, PX, width):
                nc.vector.tensor_copy(out=picked[i][:, at : at + width],
                                      in_=pages[TILES * g + i][:].indirect(list3[:, at // 16 : (at + width) // 16]))

        def spread_bias(g, hf, i):
            x_banks[hf] = bank()
            tile_no = TILES * g + i
            for jb in range(BLOCKS):
                transpose_into(x_banks[hf][:, jb * P : (jb + 1) * P],
                               bx_cols[:, tile_no : tile_no + 1].to_broadcast([P, P]), jb == 0, False)

        def add_picked(hf, i):
            if i == 0:
                x_turned[hf] = ring.tile([P, BLOCKS, PASS], BF16, name="x_turned", tag="x_turned")
            for jb in range(BLOCKS):
                src = hf * HALF + jb * P
                transpose_into(x_banks[hf][:, jb * P : (jb + 1) * P], picked[i][:, src : src + P], False, jb == BLOCKS - 1)
            round_sorted(x_turned[hf], i, x_banks[hf])

        def turn_x(g, i):
            for hf in range(2):
                spread_bias(g, hf, i)
                add_picked(hf, i)

        def turn_page(g, i, quarter):
            if i == 0:
                page_turned[quarter] = ring.tile([P, BLOCKS, PASS], BF16, name="page_turned", tag="page_turned", bufs=QUARTERS)
            page_ps = bank()
            for b in range(BLOCKS):
                src = (BLOCKS * quarter + b) * P
                nc.tensor.transpose(page_ps[:, b * P : (b + 1) * P], pages[TILES * g + i][:, src : src + P], ident[:])
            round_sorted(page_turned[quarter], i, page_ps)

        def finish_x(g, hf):
            quantize(xq[g, hf][:], xs[g, hf][:], turn_back(x_turned[hf])[:])

        page_q, page_s = {}, {}

        def finish_page(g, quarter):
            if quarter == 0:
                page_q[g] = ring.tile([P, T2], U32, name="page_q", tag="page_q", bufs=1, align_bytes=64)
                page_s[g] = ring.tile([P, T2], U8, name="page_s", tag="page_s", bufs=1, align_bytes=64)
            columns = slice(quarter * BANK, (quarter + 1) * BANK)
            quantize(page_q[g][:, columns], page_s[g][:, columns], turn_back(page_turned[quarter])[:])
            nc.sync.dma_start(out=words_of(out_2[g])[:, columns], in_=page_q[g][:, columns].bitcast(I32))
            if quarter == QUARTERS - 1:
                for q in range(4):
                    nc.sync.dma_start(out=out_3[g, 4 * q : 4 * q + 4, :].bitcast(I32),
                                      in_=page_s[g][32 * q : 32 * q + 4, :].bitcast(I32))

        sums, gated = {}, {}

        def second_pass(hf, nt, g):
            if g == 0:
                sums[hf, nt] = (bank(), bank())
            y1_ps, y2_ps = sums[hf, nt]
            outs = slice(nt * P, (nt + 1) * P)
            nc.tensor.matmul_mx(out=y1_ps[:], lhsT=w3w[:, g, 2 * nt * P : 2 * (nt + 1) * P].bitcast(FP4X4),
                                lhsT_scale=w3s[:, g, outs], rhs=xq[g, hf][:].bitcast(FP8X4), rhs_scale=xs[g, hf][:],
                                start=(g == 0), stop=(g == GROUPS - 1))
            nc.tensor.matmul_mx(out=y2_ps[:], lhsT=w4q[g][:, outs].bitcast(FP8X4), lhsT_scale=w4s[g][:, outs],
                                rhs=xq[g, hf][:].bitcast(FP8X4), rhs_scale=xs[g, hf][:],
                                start=(g == 0), stop=(g == GROUPS - 1))

        def gate(hf, nt):
            y1_ps, y2_ps = sums[hf, nt]
            th = ring.tile([P, BANK], F32, name="th", tag="sq", bufs=BLOCKS)
            nc.scalar.activation(out=th[:], in_=y1_ps[:], func=ACT.Tanh)
            gated[hf, nt] = ring.tile([P, BANK], F32, name="gated", tag="bt", bufs=BLOCKS)
            nc.vector.tensor_tensor(out=gated[hf, nt][:], in0=y2_ps[:], in1=th[:], op=ALU.mult)

        def finish_y(hf, nt):
            y = ring.tile([P, BANK], F32, name="y", tag="h", bufs=2 * TILES)
            nc.vector.tensor_tensor(out=y[:], in0=sums[hf, nt][0][:], in1=gated[hf, nt][:], op=ALU.add)
            nc.sync.dma_start(out=out_0[nt * P : (nt + 1) * P, hf * HALF : (hf + 1) * HALF], in_=y[:])

        last = TILES - 1
        every_block = range(BLOCKS)

        gather_table(0)
        prepare_w1_first()
        to_columns(gain_cols, gain_rows)
        gather_table(1)
        square_a(0, 0, every_block, range(0, 1))
        copy_b(0, 0, every_block, range(0, 1))
        copy_b(0, 0, every_block, range(1, 2))
        make_h(0, 0, 0)
        prepare_w1_rest()
        for i in range(2, TILES):
            copy_b(0, 0, every_block, range(i, i + 1))
        for i in range(1, TILES):
            square_a(0, 0, every_block, range(i, i + 1))
        for i in range(1, TILES):
            make_h(0, 0, i)
        prepare_w1_second()
        products(0, 1)
        for i in range(TILES):
            make_h(0, 1, i)
        to_columns(bx_cols, bx_rows)
        for i in range(TILES):
            scatter(0, 0, i)
        load_page(PAGE_BUFS)
        load_page(PAGE_BUFS + 1)
        products(1, 0)
        for i in range(TILES):
            make_h(1, 0, i)
        products(1, 1)

        def complete_tiles(g):
            final = g == GROUPS - 1
            for i in range(TILES):
                if i == last:
                    pick(g, i - 1, 1)
                    turn_x(g, i - 1)
                scatter(g, 1, i)
                store_page(TILES * g + i)
                if not (final and i == last):
                    for quarter in range(QUARTERS):
                        turn_page(g, i, quarter)
                if 0 < i < last:
                    pick(g, i - 1, 1)
                    turn_x(g, i - 1)
                if g == 0 and i == 1:
                    load_page(GROUPS * TILES - 1)
            pick(g, last, 2 if final else 1)

        complete_tiles(0)
        turn_x(0, last)
        for i in range(TILES):
            make_h(1, 1, i)
        for i in range(TILES):
            scatter(1, 0, i)
        for g in range(GROUPS):
            prepare_w4(g)
        for hf in range(2):
            finish_x(0, hf)
        for quarter in range(QUARTERS):
            finish_page(0, quarter)
        complete_tiles(1)

        for hf in range(2):
            spread_bias(1, hf, last)
        turn_page(1, last, 0)
        for hf in range(2):
            turn_page(1, last, 1 + hf)
            add_picked(hf, last)
        finish_x(1, 0)
        steps = [(hf, nt) for hf in range(2) for nt in range(N // P)]
        early = steps[:2]
        for hf, nt in early:
            second_pass(hf, nt, 0)
        turn_page(1, last, QUARTERS - 1)

        for n, (hf, nt) in enumerate(steps):
            if (hf, nt) not in early:
                second_pass(hf, nt, 0)
            second_pass(hf, nt, 1)
            gate(hf, nt)
            if n > 0:
                finish_y(*steps[n - 1])
            if n == len(early) - 1:
                finish_x(1, 1)
            if n >= len(early) and n % 2 == 0:
                finish_page(1, (n - len(early)) // 2)
        finish_y(*steps[-1])
